import numpy as np
import ml_dtypes


def mxq(x, axis, fmt="e4m3"):
    dtype, down = {"e4m3": (ml_dtypes.float8_e4m3fn, 7), "e5m2": (ml_dtypes.float8_e5m2, 14)}[fmt]
    v = np.moveaxis(np.asarray(x, np.float32).astype(ml_dtypes.bfloat16).astype(np.float64), axis, -1)
    blocks = v.reshape(v.shape[:-1] + (-1, 32))
    amax = np.abs(blocks).max(-1, keepdims=True)
    byte = np.maximum(np.where(amax > 0, np.frexp(amax)[1] - 1 + 127, 0) - down, 1)
    scale = np.exp2(byte - 127.0)
    codes = (blocks / scale).astype(np.float32).astype(dtype).astype(np.float64)
    return np.moveaxis((codes * scale).reshape(v.shape), -1, axis)


WIDE = False


def mx_kscale(k):
    if not WIDE:
        return np.ones(k)
    levels = np.array([18, -18])
    if k % 512:
        return np.exp2(np.random.permutation(np.resize(levels, k // 32))).repeat(32)
    a = np.empty((k // 512, 16))
    for p in range(k // 512):
        a[p, :8] = np.random.permutation(np.resize(levels, 8))
        for g in range(8):
            far = levels[np.abs(levels - a[p, g]) >= 10]
            a[p, g + 8] = far[np.random.randint(len(far))]
    return np.exp2(a.ravel()).repeat(32)


def f64(x):
    return np.asarray(x).astype(np.float64)


def striped(idx):
    return np.tile(np.asarray(idx).reshape(-1, 16).T, (8, 1)).astype(np.uint16)


def unstriped(offs):
    return offs[:16].T.reshape(-1).astype(np.int64)

def planes(y):
    n, m = y.shape
    v = y.astype(np.float32).astype(ml_dtypes.bfloat16).astype(np.float64).reshape(n // 32, 32, m)
    top = np.abs(v).max(1)
    byte = np.clip(np.where(top > 0, np.frexp(top)[1] - 1 + 127 - 7, 1), 1, 254)
    codes = (v * np.exp2(127.0 - byte)[:, None, :]).reshape(n, m).astype(np.float32).astype(ml_dtypes.float8_e4m3fn).view(np.uint8)
    words = codes.reshape(n // 512, 128, 4, m).transpose(0, 1, 3, 2)
    return np.ascontiguousarray(words), np.ascontiguousarray(byte.astype(np.uint8).reshape(n // 512, 16, m))


N, C, D, R = 1024, 4096, 512, 512


def eight(codes):
    return np.concatenate([codes[h].reshape(-1, 16).T for h in range(8)]).astype(np.uint16)


def uneight(offs):
    return np.stack([offs[16 * h:16 * h + 16].T.reshape(-1) for h in range(8)]).astype(np.int64)


def setup_inputs():
    n = np.random.standard_normal
    s = mx_kscale(D)[:, None]
    u = mx_kscale(N)
    grid = lambda x: np.round(x * 32) / 32
    return {
        "xT": (n((D, R)) * (1.0 / np.sqrt(D)) * s).astype(np.float32),
        "cb": (grid(n((D, C))) / s).astype(np.float32),
        "norm": np.tile(np.random.randint(32, 129, N) / 64.0 / u, (128, 1)).astype(np.float32),
        "ts": np.tile(np.random.uniform(0.5, 1.5, N) * u, (128, 1)).astype(np.float32),
        "y": n((R, N)).astype(np.float32),
        "wt": (np.random.uniform(0.5, 1.5, (R, 1)) * 1.0 / np.sqrt(N)).astype(np.float32),
        "offs": eight(np.random.randint(0, C, (8, N))),
    }


def reference(xT, cb, norm, ts, y, wt, offs):
    code = uneight(offs)
    k = np.concatenate([f64(cb)[64 * h:64 * h + 64][:, code[h]] for h in range(8)]) * f64(norm)[:1]
    a = f64(ts)[:1] * (mxq(f64(xT), 0, "e4m3").T @ mxq(k, 0, "e4m3"))
    g = f64(wt) * np.tanh(a - f64(y))
    h = f64(ts)[:1] * g
    out_0 = mxq(h, 1, "e5m2") @ mxq(k, 1, "e4m3").T
    return (out_0,) + planes(out_0)

@@ -1,0 +1,253 @@
+from contextlib import ExitStack
+
+import concourse.mybir as mybir
+from concourse.masks import make_identity
+
+N, C, D, R = 1024, 4096, 512, 512
+FLOPS = 2 * 2 * R * N * D
+
+F32 = mybir.dt.float32
+BF16 = mybir.dt.bfloat16
+U32 = mybir.dt.uint32
+I32 = mybir.dt.int32
+U16 = mybir.dt.uint16
+U8 = mybir.dt.uint8
+E4 = mybir.dt.float8_e4m3fn_x4
+E5 = mybir.dt.float8_e5m2_x4
+MULT = mybir.AluOpType.mult
+ACT = mybir.ActivationFunctionType
+
+P = 128
+PACK = 4
+PASS = P * PACK
+G = N // PASS
+
+
+def tile_attend_gpq_pl_lch_x_kernel(tc, xT, cb, norm, ts, y, wt, offs, out_0, out_1, out_2):
+    nc = tc.nc
+    with ExitStack() as ctx:
+        keep = ctx.enter_context(tc.tile_pool(name="keep", bufs=1))
+        ring = ctx.enter_context(tc.tile_pool(name="ring", bufs=3))
+        psum = ctx.enter_context(tc.psum_pool(name="psum", bufs=1))
+
+        def held(name, shape, dtype, tag=""):
+            return keep.tile(shape, dtype, name=name, tag=tag or name, align_bytes=64)
+
+        def bank_tile(name, shape, tag):
+            return psum.tile(shape, F32, name=name, tag=tag)
+
+        offsets = keep.tile([P, N // 16], U16, name="offsets")
+        norm_col = held("norm_col", [P, G, PACK], F32)
+        ts_col = held("ts_col", [P, G, PACK], F32)
+        wt_col = held("wt_col", [P, PACK], F32)
+        nc.sync.dma_start(out=wt_col[:], in_=wt.rearrange("(p j) o -> p (j o)", j=PACK))
+        nc.sync.dma_start(out=ts_col[:], in_=ts[0, :].rearrange("(g p t) -> p g t", g=G, t=PACK))
+
+        cb_rows = cb.rearrange("(p t) c -> p t c", t=PACK)
+        planes = [held("plane%d" % t, [P, C], F32) for t in range(PACK)]
+        x_raw = held("x_raw", [P, PACK, R], F32)
+        y_rows = y.rearrange("(p j) n -> p j n", j=PACK)
+        y_raw = [held("y_raw%d" % j, [P, N], F32) for j in range(PACK)]
+        nc.sync.dma_start(out=planes[0][:], in_=cb_rows[:, 0, :])
+        nc.sync.dma_start(offsets[:], offs)
+        nc.sync.dma_start(out=norm_col[:], in_=norm[0, :].rearrange("(g p t) -> p g t", g=G, t=PACK))
+        for t in range(1, PACK - 1):
+            nc.sync.dma_start(out=planes[t][:], in_=cb_rows[:, t, :])
+        nc.sync.dma_start(out=x_raw[:], in_=xT.rearrange("(p t) r -> p t r", t=PACK))
+        nc.sync.dma_start(out=planes[PACK - 1][:], in_=cb_rows[:, PACK - 1, :])
+        for j in range(PACK):
+            nc.sync.dma_start(out=y_raw[j][:], in_=y_rows[:, j, :])
+
+        ident = held("ident", [P, P], F32)
+        make_identity(nc, ident[:])
+        warm = held("warm", [P, 8], F32)
+        nc.scalar.activation(out=warm[:], in_=ident[:, 0:8], func=ACT.Tanh)
+
+        def spread(columns, tag):
+            bank = bank_tile("spread", [P, PACK, P], tag)
+            for t in range(PACK):
+                nc.tensor.transpose(bank[:, t, :], columns[:, t:t + 1].to_broadcast([P, P]), ident[:])
+            return bank
+
+        norm_row = [held("norm_row%d" % g, [P, PASS], F32) for g in range(G)]
+        neg_ts_row = [held("neg_ts_row%d" % g, [P, PACK, P], F32) for g in range(G)]
+        for g in range(G):
+            bank = spread(norm_col[:, g, :], "s%d" % g)
+            nc.scalar.copy(out=norm_row[g][:].rearrange("q (s t) -> q s t", t=PACK), in_=bank[:].rearrange("q t s -> q s t"))
+        wt_bank = spread(wt_col, "a2")
+        tw = [held("tw%d" % j, [P, G, P, PACK], F32) for j in range(PACK)]
+        for j in range(PACK):
+            nc.vector.tensor_tensor(
+                out=tw[j][:],
+                in0=wt_bank[:, j, :].unsqueeze(1).unsqueeze(3).to_broadcast([P, G, P, PACK]),
+                in1=ts_col[:].unsqueeze(2).to_broadcast([P, G, P, PACK]),
+                op=MULT)
+        for g in range(G):
+            bank = spread(ts_col[:, g, :], "a%d" % g)
+            nc.scalar.activation(out=neg_ts_row[g][:], in_=bank[:], func=ACT.Copy, scale=-1.0)
+
+        k_f32 = [[held("k_f32_%d_%d" % (h, g), [P, 2, PASS], F32) for g in range(G)] for h in range(2)]
+        kd_in = [held("kd_in%d" % g, [P, PASS, PACK], BF16) for g in range(G)]
+        kd_codes = [held("kd_codes%d" % g, [P, PASS], U32) for g in range(G)]
+        kd_scales = [held("kd_scales%d" % g, [P, PASS], U8) for g in range(G)]
+        kn_codes = [held("kn_codes%d" % g, [P, D], U32) for g in range(G)]
+        kn_scales = [held("kn_scales%d" % g, [P, D], U8) for g in range(G)]
+
+        def gather(t, g):
+            cols = PASS // 16
+            nc.vector.tensor_tensor(
+                out=k_f32[t // 2][g][:, t % 2, :],
+                in0=planes[t][:].indirect(offsets[:, g * cols:(g + 1) * cols]),
+                in1=norm_row[g][:], op=MULT)
+
+        def weave_pair(h, g, copy):
+            copy(out=kd_in[g][:, :, 2 * h:2 * h + 2], in_=k_f32[h][g][:].rearrange("p e n -> p n e"))
+
+        def quantize_kd(g):
+            nc.vector.quantize_mx(out=kd_codes[g][:].bitcast(E4), scales=kd_scales[g][:],
+                                  in_=kd_in[g][:].rearrange("p n t -> p (n t)"))
+
+        def turn_k(t, g):
+            bank = bank_tile("k_bank", [P, PACK, P], ("z%d" if t % 2 == 0 else "a%d") % g)
+            src = k_f32[t // 2][g][:, t % 2, :].rearrange("p (s u) -> p u s", u=PACK)
+            for u in range(PACK):
+                nc.tensor.transpose(bank[:, u, :], src[:, u, :], ident[:])
+            kn_in = ring.tile([P, P, PACK], BF16, name="kn_in", align_bytes=64)
+            nc.scalar.copy(out=kn_in[:], in_=bank[:].rearrange("s u p -> s p u"))
+            return kn_in
+
+        def quantize_kn(t, g, kn_in):
+            cols = slice(t * P, (t + 1) * P)
+            nc.vector.quantize_mx(out=kn_codes[g][:, cols].bitcast(E4), scales=kn_scales[g][:, cols],
+                                  in_=kn_in[:].rearrange("s p u -> s (p u)"))
+
+        x_codes = held("x_codes", [P, R], U32)
+        x_scales = held("x_scales", [P, R], U8)
+
+        for t in range(PACK - 1):
+            for g in range(G):
+                gather(t, g)
+            for g in range(G):
+                quantize_kn(t, g, turn_k(t, g))
+            if t == 1:
+                for g in range(G):
+                    weave_pair(0, g, nc.scalar.copy)
+        x_in = held("x_in", [P, PACK, P, PACK], BF16, tag="k_f32_0_1")
+        nc.scalar.copy(out=x_in[:].rearrange("p j m t -> p m j t"), in_=x_raw[:].rearrange("p t (m j) -> p m j t", j=PACK))
+        nc.vector.quantize_mx(out=x_codes[:].bitcast(E4), scales=x_scales[:], in_=x_in[:].rearrange("p j m t -> p (j m t)"))
+
+        y_dealt = {}
+        deal_tags = ["x_raw", "k_f32_0_0", "k_f32_1_0", "k_f32_1_1"]
+
+        def deal_y(j):
+            dealt = held("y_dealt", [P, G, PACK, P], F32, tag=deal_tags[j])
+            nc.scalar.copy(out=dealt[:].rearrange("p g u s -> p g s u"), in_=y_raw[j][:].rearrange("p (g s u) -> p g s u", g=G, u=PACK))
+            y_dealt[j] = dealt
+
+        last = PACK - 1
+        gather(last, 0)
+        gather(last, 1)
+        deal_y(0)
+        weave_pair(1, 0, nc.scalar.copy)
+        weave_pair(1, 1, nc.vector.tensor_copy)
+        quantize_kd(1)
+        quantize_kd(0)
+        turned = [turn_k(last, g) for g in range(G)]
+
+        units = [(j, g) for j in range(PACK) for g in (1, 0)]
+
+        z_banks, s_banks, neg_a, th, h_in, h_codes, h_scales, accs = {}, {}, {}, {}, {}, {}, {}, {}
+
+        def turn_y(i):
+            j, g = units[i]
+            z_banks[i] = bank_tile("z_bank", [P, PACK, P], "z%d" % (i % 3))
+            for u in range(PACK):
+                nc.tensor.matmul(z_banks[i][:, u, :], lhsT=y_dealt[j][:, g, u, :], rhs=ident[:], is_transpose=True, start=(u == 0), stop=False)
+
+        def score(i):
+            j, g = units[i]
+            cols = slice(j * P, (j + 1) * P)
+            s_banks[i] = bank_tile("s_bank", [P, PASS], "s%d" % (i % 2))
+            nc.tensor.matmul_mx(out=s_banks[i][:], lhsT=x_codes[:, cols].bitcast(E4), lhsT_scale=x_scales[:, cols],
+                                rhs=kd_codes[g][:].bitcast(E4), rhs_scale=kd_scales[g][:], start=True, stop=True)
+
+        def scale_scores(i):
+            j, g = units[i]
+            neg_a[i] = ring.tile([P, PACK, P], F32, name="neg_a", align_bytes=64)
+            nc.vector.tensor_tensor(out=neg_a[i][:], in0=s_banks[i][:].rearrange("p (s u) -> p u s", u=PACK), in1=neg_ts_row[g][:], op=MULT)
+
+        def turn_a(i):
+            for u in range(PACK):
+                nc.tensor.matmul(z_banks[i][:, u, :], lhsT=neg_a[i][:, u, :], rhs=ident[:], is_transpose=True, start=False, stop=(u == PACK - 1))
+
+        def squash(i):
+            th[i] = ring.tile([P, P, PACK], F32, name="th", align_bytes=64)
+            nc.scalar.activation(out=th[i][:], in_=z_banks[i][:].rearrange("s u p -> s p u"), func=ACT.Tanh, scale=-1.0)
+
+        def weigh(i):
+            j, g = units[i]
+            h_in[i] = ring.tile([P, P, PACK], BF16, name="h_in", align_bytes=64)
+            nc.vector.tensor_tensor(out=h_in[i][:], in0=th[i][:], in1=tw[j][:, g, :, :], op=MULT)
+
+        def quantize_h(i):
+            h_codes[i] = ring.tile([P, P], U32, name="h_codes", align_bytes=64)
+            h_scales[i] = ring.tile([P, P], U8, name="h_scales", align_bytes=64)
+            nc.vector.quantize_mx(out=h_codes[i][:].bitcast(E5), scales=h_scales[i][:], in_=h_in[i][:].rearrange("s p u -> s (p u)"))
+
+        out_f32 = [held("out_f32_%d" % h, [P, 2, D], F32) for h in range(2)]
+        out_in = held("out_in", [P, D, PACK], BF16)
+        out_rows = out_0.rearrange("(p j) d -> p j d", j=PACK)
+
+        def back(i):
+            j, g = units[i]
+            if g == 1:
+                accs[j] = bank_tile("acc", [P, D], "a%d" % ((j + 2) % 3))
+            nc.tensor.matmul_mx(out=accs[j][:], lhsT=h_codes[i][:].bitcast(E5), lhsT_scale=h_scales[i][:],
+                                rhs=kn_codes[g][:].bitcast(E4), rhs_scale=kn_scales[g][:], start=(g == 1), stop=(g == 0))
+            if g == 0:
+                h = j // 2
+                parts = 2 if j == PACK - 1 else 1
+                width = D // parts
+                for part in range(parts):
+                    cols = slice(part * width, (part + 1) * width)
+                    nc.scalar.copy(out=out_f32[h][:, j % 2, cols].rearrange("q (p t) -> q p t", t=PACK),
+                                   in_=accs[j][:].rearrange("q (t p) -> q p t", t=PACK)[:, part * width // PACK:(part + 1) * width // PACK, :])
+                    if j % 2 == 1:
+                        nc.vector.tensor_copy(out=out_in[:, cols, 2 * h:2 * h + 2], in_=out_f32[h][:, :, cols].rearrange("q e d -> q d e"))
+                nc.sync.dma_start(out=out_rows[:, j, :], in_=out_f32[h][:, j % 2, :])
+
+        count = len(units)
+        turn_y(0)
+        turn_y(1)
+        for step in range(count + 4):
+            if step < count:
+                score(step)
+            if 0 <= step - 1 < count:
+                turn_a(step - 1)
+            if step < count:
+                scale_scores(step)
+            if step < G:
+                quantize_kn(last, 1 - step, turned[1 - step])
+            if 0 <= step - 3 < count:
+                quantize_h(step - 3)
+            if 0 <= step - 2 < count:
+                weigh(step - 2)
+            if 0 <= step - 1 < count:
+                squash(step - 1)
+            if step % G == 0 and step // G + 1 < PACK:
+                deal_y(step // G + 1)
+            if step + 2 < count:
+                turn_y(step + 2)
+            if 0 <= step - 4 < count:
+                back(step - 4)
+
+        out_codes = held("out_codes", [P, D], U32)
+        out_scales = held("out_scales", [P, D], U8)
+        words = out_1[0].rearrange("p d l -> p (d l)").bitcast(I32)
+        for part in range(2):
+            cols = slice(part * D // 2, (part + 1) * D // 2)
+            nc.vector.quantize_mx(out=out_codes[:, cols].bitcast(E4), scales=out_scales[:, cols], in_=out_in[:, cols, :].rearrange("q d j -> q (d j)"))
+            nc.scalar.dma_start(out=words[:, cols], in_=out_codes[:, cols].bitcast(I32))
+        for q in range(4):
+            queue = nc.scalar if q % 2 else nc.sync
+            queue.dma_start(out=out_2[0, 4 * q:4 * q + 4, :].bitcast(I32), in_=out_scales[32 * q:32 * q + 4, :].bitcast(I32))

@@ -51,10 +51,10 @@ def tile_attend_gpq_pl_lch_x_kernel(tc, xT, cb, norm, ts, y, wt, offs, out_0, ou
         nc.sync.dma_start(out=planes[0][:], in_=cb_rows[:, 0, :])
         nc.sync.dma_start(offsets[:], offs)
         nc.sync.dma_start(out=norm_col[:], in_=norm[0, :].rearrange("(g p t) -> p g t", g=G, t=PACK))
-        for t in range(1, PACK - 1):
-            nc.sync.dma_start(out=planes[t][:], in_=cb_rows[:, t, :])
+        nc.sync.dma_start(out=planes[1][:], in_=cb_rows[:, 1, :])
         nc.sync.dma_start(out=x_raw[:], in_=xT.rearrange("(p t) r -> p t r", t=PACK))
-        nc.sync.dma_start(out=planes[PACK - 1][:], in_=cb_rows[:, PACK - 1, :])
+        for t in range(2, PACK):
+            nc.sync.dma_start(out=planes[t][:], in_=cb_rows[:, t, :])
         for j in range(PACK):
             nc.sync.dma_start(out=y_raw[j][:], in_=y_rows[:, j, :])
 
@@ -74,7 +74,7 @@ def tile_attend_gpq_pl_lch_x_kernel(tc, xT, cb, norm, ts, y, wt, offs, out_0, ou
         for g in range(G):
             bank = spread(norm_col[:, g, :], "s%d" % g)
             nc.scalar.copy(out=norm_row[g][:].rearrange("q (s t) -> q s t", t=PACK), in_=bank[:].rearrange("q t s -> q s t"))
-        wt_bank = spread(wt_col, "a2")
+        wt_bank = spread(wt_col, "z2")
         tw = [held("tw%d" % j, [P, G, P, PACK], F32) for j in range(PACK)]
         for j in range(PACK):
             nc.vector.tensor_tensor(
@@ -88,6 +88,7 @@ def tile_attend_gpq_pl_lch_x_kernel(tc, xT, cb, norm, ts, y, wt, offs, out_0, ou
 
         k_f32 = [[held("k_f32_%d_%d" % (h, g), [P, 2, PASS], F32) for g in range(G)] for h in range(2)]
         kd_in = [held("kd_in%d" % g, [P, PASS, PACK], BF16) for g in range(G)]
+        kn_in = [[held("kn_in_%d_%d" % (h, g), [P, 2, P, PACK], BF16) for g in range(G)] for h in range(2)]
         kd_codes = [held("kd_codes%d" % g, [P, PASS], U32) for g in range(G)]
         kd_scales = [held("kd_scales%d" % g, [P, PASS], U8) for g in range(G)]
         kn_codes = [held("kn_codes%d" % g, [P, D], U32) for g in range(G)]
@@ -112,29 +113,28 @@ def tile_attend_gpq_pl_lch_x_kernel(tc, xT, cb, norm, ts, y, wt, offs, out_0, ou
             src = k_f32[t // 2][g][:, t % 2, :].rearrange("p (s u) -> p u s", u=PACK)
             for u in range(PACK):
                 nc.tensor.transpose(bank[:, u, :], src[:, u, :], ident[:])
-            kn_in = ring.tile([P, P, PACK], BF16, name="kn_in", align_bytes=64)
-            nc.scalar.copy(out=kn_in[:], in_=bank[:].rearrange("s u p -> s p u"))
-            return kn_in
+            nc.scalar.copy(out=kn_in[t // 2][g][:, t % 2, :, :], in_=bank[:].rearrange("s u p -> s p u"))
 
-        def quantize_kn(t, g, kn_in):
-            cols = slice(t * P, (t + 1) * P)
+        def quantize_kn(h, g):
+            cols = slice(2 * h * P, 2 * (h + 1) * P)
             nc.vector.quantize_mx(out=kn_codes[g][:, cols].bitcast(E4), scales=kn_scales[g][:, cols],
-                                  in_=kn_in[:].rearrange("s p u -> s (p u)"))
+                                  in_=kn_in[h][g][:].rearrange("s e p u -> s (e p u)"))
 
         x_codes = held("x_codes", [P, R], U32)
         x_scales = held("x_scales", [P, R], U8)
 
+        x_in = held("x_in", [P, PACK, P, PACK], BF16)
         for t in range(PACK - 1):
             for g in range(G):
                 gather(t, g)
             for g in range(G):
-                quantize_kn(t, g, turn_k(t, g))
+                turn_k(t, g)
             if t == 1:
+                nc.vector.tensor_copy(out=x_in[:].rearrange("p j m t -> p m j t"), in_=x_raw[:].rearrange("p t (m j) -> p m j t", j=PACK))
                 for g in range(G):
+                    quantize_kn(0, g)
                     weave_pair(0, g, nc.scalar.copy)
-        x_in = held("x_in", [P, PACK, P, PACK], BF16, tag="k_f32_0_1")
-        nc.scalar.copy(out=x_in[:].rearrange("p j m t -> p m j t"), in_=x_raw[:].rearrange("p t (m j) -> p m j t", j=PACK))
-        nc.vector.quantize_mx(out=x_codes[:].bitcast(E4), scales=x_scales[:], in_=x_in[:].rearrange("p j m t -> p (j m t)"))
+                nc.vector.quantize_mx(out=x_codes[:].bitcast(E4), scales=x_scales[:], in_=x_in[:].rearrange("p j m t -> p (j m t)"))
 
         y_dealt = {}
         deal_tags = ["x_raw", "k_f32_0_0", "k_f32_1_0", "k_f32_1_1"]
@@ -148,98 +148,138 @@ def tile_attend_gpq_pl_lch_x_kernel(tc, xT, cb, norm, ts, y, wt, offs, out_0, ou
         gather(last, 0)
         gather(last, 1)
         deal_y(0)
-        weave_pair(1, 0, nc.scalar.copy)
+        weave_pair(1, 0, nc.vector.tensor_copy)
         weave_pair(1, 1, nc.vector.tensor_copy)
-        quantize_kd(1)
         quantize_kd(0)
-        turned = [turn_k(last, g) for g in range(G)]
-
-        units = [(j, g) for j in range(PACK) for g in (1, 0)]
-
+        quantize_kd(1)
+        order = (0, 1)
         z_banks, s_banks, neg_a, th, h_in, h_codes, h_scales, accs = {}, {}, {}, {}, {}, {}, {}, {}
 
-        def turn_y(i):
-            j, g = units[i]
-            z_banks[i] = bank_tile("z_bank", [P, PACK, P], "z%d" % (i % 3))
+        def turn_y(j, g):
+            z_banks[j, g] = bank_tile("z_bank", [P, PACK, P], "z%d" % (2 * (j % 2) + g))
             for u in range(PACK):
-                nc.tensor.matmul(z_banks[i][:, u, :], lhsT=y_dealt[j][:, g, u, :], rhs=ident[:], is_transpose=True, start=(u == 0), stop=False)
+                nc.tensor.matmul(z_banks[j, g][:, u, :], lhsT=y_dealt[j][:, g, u, :], rhs=ident[:], is_transpose=True, start=(u == 0), stop=False)
 
-        def score(i):
-            j, g = units[i]
+        def score(j, g):
             cols = slice(j * P, (j + 1) * P)
-            s_banks[i] = bank_tile("s_bank", [P, PASS], "s%d" % (i % 2))
-            nc.tensor.matmul_mx(out=s_banks[i][:], lhsT=x_codes[:, cols].bitcast(E4), lhsT_scale=x_scales[:, cols],
+            s_banks[j, g] = bank_tile("s_bank", [P, PASS], "s%d" % g)
+            nc.tensor.matmul_mx(out=s_banks[j, g][:], lhsT=x_codes[:, cols].bitcast(E4), lhsT_scale=x_scales[:, cols],
                                 rhs=kd_codes[g][:].bitcast(E4), rhs_scale=kd_scales[g][:], start=True, stop=True)
 
-        def scale_scores(i):
-            j, g = units[i]
-            neg_a[i] = ring.tile([P, PACK, P], F32, name="neg_a", align_bytes=64)
-            nc.vector.tensor_tensor(out=neg_a[i][:], in0=s_banks[i][:].rearrange("p (s u) -> p u s", u=PACK), in1=neg_ts_row[g][:], op=MULT)
+        def scale_scores(j, g):
+            neg_a[j, g] = ring.tile([P, PACK, P], F32, name="neg_a", align_bytes=64, bufs=4)
+            nc.vector.tensor_tensor(out=neg_a[j, g][:], in0=s_banks[j, g][:].rearrange("p (s u) -> p u s", u=PACK), in1=neg_ts_row[g][:], op=MULT)
 
-        def turn_a(i):
+        def turn_a(j, g):
             for u in range(PACK):
-                nc.tensor.matmul(z_banks[i][:, u, :], lhsT=neg_a[i][:, u, :], rhs=ident[:], is_transpose=True, start=False, stop=(u == PACK - 1))
+                nc.tensor.matmul(z_banks[j, g][:, u, :], lhsT=neg_a[j, g][:, u, :], rhs=ident[:], is_transpose=True, start=False, stop=(u == PACK - 1))
 
-        def squash(i):
-            th[i] = ring.tile([P, P, PACK], F32, name="th", align_bytes=64)
-            nc.scalar.activation(out=th[i][:], in_=z_banks[i][:].rearrange("s u p -> s p u"), func=ACT.Tanh, scale=-1.0)
+        def squash(j, g):
+            if g == order[0]:
+                th[j] = ring.tile([P, G, P, PACK], F32, name="th", align_bytes=64)
+            nc.scalar.activation(out=th[j][:, g, :, :], in_=z_banks[j, g][:].rearrange("s u p -> s p u"), func=ACT.Tanh, scale=-1.0)
 
-        def weigh(i):
-            j, g = units[i]
-            h_in[i] = ring.tile([P, P, PACK], BF16, name="h_in", align_bytes=64)
-            nc.vector.tensor_tensor(out=h_in[i][:], in0=th[i][:], in1=tw[j][:, g, :, :], op=MULT)
+        def weigh(j, gs):
+            if j not in h_in:
+                h_in[j] = ring.tile([P, G, P, PACK], BF16, name="h_in", align_bytes=64)
+            nc.vector.tensor_tensor(out=h_in[j][:, gs, :, :], in0=th[j][:, gs, :, :], in1=tw[j][:, gs, :, :], op=MULT)
 
-        def quantize_h(i):
-            h_codes[i] = ring.tile([P, P], U32, name="h_codes", align_bytes=64)
-            h_scales[i] = ring.tile([P, P], U8, name="h_scales", align_bytes=64)
-            nc.vector.quantize_mx(out=h_codes[i][:].bitcast(E5), scales=h_scales[i][:], in_=h_in[i][:].rearrange("s p u -> s (p u)"))
+        def quantize_h(j, gs):
+            if j not in h_codes:
+                h_codes[j] = ring.tile([P, G, P], U32, name="h_codes", align_bytes=64)
+                h_scales[j] = ring.tile([P, G, P], U8, name="h_scales", align_bytes=64)
+            nc.vector.quantize_mx(out=h_codes[j][:, gs, :].rearrange("s g p -> s (g p)").bitcast(E5),
+                                  scales=h_scales[j][:, gs, :].rearrange("s g p -> s (g p)"),
+                                  in_=h_in[j][:, gs, :, :].rearrange("s g p u -> s (g p u)"))
 
         out_f32 = [held("out_f32_%d" % h, [P, 2, D], F32) for h in range(2)]
         out_in = held("out_in", [P, D, PACK], BF16)
         out_rows = out_0.rearrange("(p j) d -> p j d", j=PACK)
 
-        def back(i):
-            j, g = units[i]
-            if g == 1:
-                accs[j] = bank_tile("acc", [P, D], "a%d" % ((j + 2) % 3))
-            nc.tensor.matmul_mx(out=accs[j][:], lhsT=h_codes[i][:].bitcast(E5), lhsT_scale=h_scales[i][:],
-                                rhs=kn_codes[g][:].bitcast(E4), rhs_scale=kn_scales[g][:], start=(g == 1), stop=(g == 0))
-            if g == 0:
-                h = j // 2
-                parts = 2 if j == PACK - 1 else 1
-                width = D // parts
-                for part in range(parts):
-                    cols = slice(part * width, (part + 1) * width)
-                    nc.scalar.copy(out=out_f32[h][:, j % 2, cols].rearrange("q (p t) -> q p t", t=PACK),
-                                   in_=accs[j][:].rearrange("q (t p) -> q p t", t=PACK)[:, part * width // PACK:(part + 1) * width // PACK, :])
-                    if j % 2 == 1:
-                        nc.vector.tensor_copy(out=out_in[:, cols, 2 * h:2 * h + 2], in_=out_f32[h][:, :, cols].rearrange("q e d -> q d e"))
-                nc.sync.dma_start(out=out_rows[:, j, :], in_=out_f32[h][:, j % 2, :])
+        def back(j, g):
+            if g == order[0]:
+                accs[j] = bank_tile("acc", [P, D], "a%d" % (j % 2))
+            nc.tensor.matmul_mx(out=accs[j][:], lhsT=h_codes[j][:, g, :].bitcast(E5), lhsT_scale=h_scales[j][:, g, :],
+                                rhs=kn_codes[g][:].bitcast(E4), rhs_scale=kn_scales[g][:], start=(g == order[0]), stop=(g == order[1]))
 
-        count = len(units)
-        turn_y(0)
-        turn_y(1)
-        for step in range(count + 4):
-            if step < count:
-                score(step)
-            if 0 <= step - 1 < count:
-                turn_a(step - 1)
-            if step < count:
-                scale_scores(step)
-            if step < G:
-                quantize_kn(last, 1 - step, turned[1 - step])
-            if 0 <= step - 3 < count:
-                quantize_h(step - 3)
-            if 0 <= step - 2 < count:
-                weigh(step - 2)
-            if 0 <= step - 1 < count:
-                squash(step - 1)
-            if step % G == 0 and step // G + 1 < PACK:
-                deal_y(step // G + 1)
-            if step + 2 < count:
-                turn_y(step + 2)
-            if 0 <= step - 4 < count:
-                back(step - 4)
+        def empty(j, part, parts):
+            width = D // parts
+            nc.scalar.copy(out=out_f32[j // 2][:, j % 2, part * width:(part + 1) * width].rearrange("q (p t) -> q p t", t=PACK),
+                           in_=accs[j][:].rearrange("q (t p) -> q p t", t=PACK)[:, part * width // PACK:(part + 1) * width // PACK, :])
+
+        def store(j):
+            nc.sync.dma_start(out=out_rows[:, j, :], in_=out_f32[j // 2][:, j % 2, :])
+
+        def weave_out(h, cols):
+            nc.vector.tensor_copy(out=out_in[:, cols, 2 * h:2 * h + 2], in_=out_f32[h][:, :, cols].rearrange("q e d -> q d e"))
+
+        def front(j):
+            for g in order:
+                scale_scores(j, g)
+
+        def middle(j):
+            for g in order:
+                turn_a(j, g)
+                squash(j, g)
+
+        def finish(j):
+            for g in order:
+                back(j, g)
+            empty(j, 0, 1)
+            store(j)
+
+        both = slice(0, G)
+        for g in order:
+            turn_y(0, g)
+        deal_y(1)
+        for g in order:
+            score(0, g)
+        for g in order:
+            turn_y(1, g)
+        deal_y(2)
+        for g in order:
+            scale_scores(0, g)
+            score(1, g)
+        middle(0)
+        deal_y(3)
+        for g in order:
+            turn_k(last, g)
+        for g in order:
+            scale_scores(1, g)
+            score(2, g)
+        middle(1)
+        for g in order:
+            turn_y(2, g)
+        weigh(0, both)
+        for g in order:
+            quantize_kn(1, g)
+        for g in order:
+            scale_scores(2, g)
+            score(3, g)
+        quantize_h(0, both)
+        middle(2)
+        finish(0)
+        for g in order:
+            turn_y(3, g)
+        weigh(1, both)
+        front(3)
+        quantize_h(1, both)
+        middle(3)
+        finish(1)
+        weigh(2, both)
+        weigh(3, slice(0, 1))
+        quantize_h(2, both)
+        weigh(3, slice(1, 2))
+        quantize_h(3, slice(0, 1))
+        finish(2)
+        quantize_h(3, slice(1, 2))
+        for g in order:
+            back(3, g)
+        weave_out(0, slice(0, D))
+        for part in range(2):
+            empty(3, part, 2)
+            weave_out(1, slice(part * D // 2, (part + 1) * D // 2))
+        store(3)
 
         out_codes = held("out_codes", [P, D], U32)
         out_scales = held("out_scales", [P, D], U8)

@@ -12,8 +12,8 @@ U32 = mybir.dt.uint32
 I32 = mybir.dt.int32
 U16 = mybir.dt.uint16
 U8 = mybir.dt.uint8
-E4 = mybir.dt.float8_e4m3fn_x4
-E5 = mybir.dt.float8_e5m2_x4
+E4M3 = mybir.dt.float8_e4m3fn_x4
+E5M2 = mybir.dt.float8_e5m2_x4
 MULT = mybir.AluOpType.mult
 ACT = mybir.ActivationFunctionType
 
@@ -21,6 +21,17 @@ P = 128
 PACK = 4
 PASS = P * PACK
 G = N // PASS
+UNITS = PACK * G
+
+SCORE_BANKS = (0, 1, 2)
+DIFF_BANKS = (3, 4, 5)
+SUM_BANKS = (6, 7)
+
+SCORE_AHEAD = 2
+SCALE_AHEAD = 1
+WEIGH_BEHIND = 2
+QUANT_BEHIND = 2
+BACK_BEHIND = 5
 
 
 def tile_attend_gpq_pl_lch_x_kernel(tc, xT, cb, norm, ts, y, wt, offs, out_0, out_1, out_2):
@@ -30,31 +41,32 @@ def tile_attend_gpq_pl_lch_x_kernel(tc, xT, cb, norm, ts, y, wt, offs, out_0, ou
         ring = ctx.enter_context(tc.tile_pool(name="ring", bufs=3))
         psum = ctx.enter_context(tc.psum_pool(name="psum", bufs=1))
 
-        def held(name, shape, dtype, tag=""):
-            return keep.tile(shape, dtype, name=name, tag=tag or name, align_bytes=64)
+        def held(name, shape, dtype, on=""):
+            return keep.tile(shape, dtype, name=name, tag=on or name, align_bytes=64)
 
-        def bank_tile(name, shape, tag):
-            return psum.tile(shape, F32, name=name, tag=tag)
+        def bank_tile(name, shape, bank):
+            return psum.tile(shape, F32, name=name, tag="bank%d" % bank)
 
-        offsets = keep.tile([P, N // 16], U16, name="offsets")
-        norm_col = held("norm_col", [P, G, PACK], F32)
-        ts_col = held("ts_col", [P, G, PACK], F32)
         wt_col = held("wt_col", [P, PACK], F32)
-        nc.sync.dma_start(out=wt_col[:], in_=wt.rearrange("(p j) o -> p (j o)", j=PACK))
-        nc.sync.dma_start(out=ts_col[:], in_=ts[0, :].rearrange("(g p t) -> p g t", g=G, t=PACK))
-
-        cb_rows = cb.rearrange("(p t) c -> p t c", t=PACK)
+        ts_col = held("ts_col", [P, G, PACK], F32)
+        norm_col = held("norm_col", [P, G, PACK], F32)
+        offsets = keep.tile([P, N // 16], U16, name="offsets")
         planes = [held("plane%d" % t, [P, C], F32) for t in range(PACK)]
-        x_raw = held("x_raw", [P, PACK, R], F32)
-        y_rows = y.rearrange("(p j) n -> p j n", j=PACK)
+        x_raw = [held("x_raw%d" % half, [P, PACK, R // 2], F32) for half in range(2)]
         y_raw = [held("y_raw%d" % j, [P, N], F32) for j in range(PACK)]
+        cb_rows = cb.rearrange("(p t) c -> p t c", t=PACK)
+        x_rows = xT.rearrange("(p t) r -> p t r", t=PACK)
+        y_rows = y.rearrange("(m j) n -> m j n", j=PACK)
+
+        nc.sync.dma_start(out=wt_col[:], in_=wt.rearrange("(m j) o -> m (j o)", j=PACK))
+        nc.sync.dma_start(out=ts_col[:], in_=ts[0, :].rearrange("(g s u) -> s g u", g=G, u=PACK))
+        nc.sync.dma_start(out=norm_col[:], in_=norm[0, :].rearrange("(g s u) -> s g u", g=G, u=PACK))
         nc.sync.dma_start(out=planes[0][:], in_=cb_rows[:, 0, :])
         nc.sync.dma_start(offsets[:], offs)
-        nc.sync.dma_start(out=norm_col[:], in_=norm[0, :].rearrange("(g p t) -> p g t", g=G, t=PACK))
-        nc.sync.dma_start(out=planes[1][:], in_=cb_rows[:, 1, :])
-        nc.sync.dma_start(out=x_raw[:], in_=xT.rearrange("(p t) r -> p t r", t=PACK))
-        for t in range(2, PACK):
+        for t in range(1, PACK):
             nc.sync.dma_start(out=planes[t][:], in_=cb_rows[:, t, :])
+        for half in range(2):
+            nc.sync.dma_start(out=x_raw[half][:], in_=x_rows[:, :, half * R // 2:(half + 1) * R // 2])
         for j in range(PACK):
             nc.sync.dma_start(out=y_raw[j][:], in_=y_rows[:, j, :])
 
@@ -63,36 +75,32 @@ def tile_attend_gpq_pl_lch_x_kernel(tc, xT, cb, norm, ts, y, wt, offs, out_0, ou
         warm = held("warm", [P, 8], F32)
         nc.scalar.activation(out=warm[:], in_=ident[:, 0:8], func=ACT.Tanh)
 
-        def spread(columns, tag):
-            bank = bank_tile("spread", [P, PACK, P], tag)
-            for t in range(PACK):
-                nc.tensor.transpose(bank[:, t, :], columns[:, t:t + 1].to_broadcast([P, P]), ident[:])
-            return bank
+        def spread(columns, bank):
+            rows = bank_tile("rows", [P, PACK, P], bank)
+            for u in range(PACK):
+                nc.tensor.transpose(rows[:, u, :], columns[:, u:u + 1].to_broadcast([P, P]), ident[:])
+            return rows
 
         norm_row = [held("norm_row%d" % g, [P, PASS], F32) for g in range(G)]
         neg_ts_row = [held("neg_ts_row%d" % g, [P, PACK, P], F32) for g in range(G)]
-        for g in range(G):
-            bank = spread(norm_col[:, g, :], "s%d" % g)
-            nc.scalar.copy(out=norm_row[g][:].rearrange("q (s t) -> q s t", t=PACK), in_=bank[:].rearrange("q t s -> q s t"))
-        wt_bank = spread(wt_col, "z2")
         tw = [held("tw%d" % j, [P, G, P, PACK], F32) for j in range(PACK)]
+        for g in range(G):
+            rows = spread(norm_col[:, g, :], SCORE_BANKS[g])
+            nc.scalar.copy(out=norm_row[g][:].rearrange("q (s u) -> q s u", u=PACK), in_=rows[:].rearrange("q u s -> q s u"))
+        wt_rows = spread(wt_col, SCORE_BANKS[2])
         for j in range(PACK):
             nc.vector.tensor_tensor(
                 out=tw[j][:],
-                in0=wt_bank[:, j, :].unsqueeze(1).unsqueeze(3).to_broadcast([P, G, P, PACK]),
+                in0=wt_rows[:, j, :].unsqueeze(1).unsqueeze(3).to_broadcast([P, G, P, PACK]),
                 in1=ts_col[:].unsqueeze(2).to_broadcast([P, G, P, PACK]),
                 op=MULT)
         for g in range(G):
-            bank = spread(ts_col[:, g, :], "a%d" % g)
-            nc.scalar.activation(out=neg_ts_row[g][:], in_=bank[:], func=ACT.Copy, scale=-1.0)
+            rows = spread(ts_col[:, g, :], DIFF_BANKS[g])
+            nc.scalar.activation(out=neg_ts_row[g][:], in_=rows[:], func=ACT.Copy, scale=-1.0)
 
-        k_f32 = [[held("k_f32_%d_%d" % (h, g), [P, 2, PASS], F32) for g in range(G)] for h in range(2)]
+        k_f32 = [[held("k_f32_%d_%d" % (pair, g), [P, 2, PASS], F32) for g in range(G)] for pair in range(2)]
         kd_in = [held("kd_in%d" % g, [P, PASS, PACK], BF16) for g in range(G)]
-        kn_in = [[held("kn_in_%d_%d" % (h, g), [P, 2, P, PACK], BF16) for g in range(G)] for h in range(2)]
-        kd_codes = [held("kd_codes%d" % g, [P, PASS], U32) for g in range(G)]
-        kd_scales = [held("kd_scales%d" % g, [P, PASS], U8) for g in range(G)]
-        kn_codes = [held("kn_codes%d" % g, [P, D], U32) for g in range(G)]
-        kn_scales = [held("kn_scales%d" % g, [P, D], U8) for g in range(G)]
+        kn_in = [[held("kn_in_%d_%d" % (pair, g), [P, 2, P, PACK], BF16) for g in range(G)] for pair in range(2)]
 
         def gather(t, g):
             cols = PASS // 16
@@ -101,192 +109,166 @@ def tile_attend_gpq_pl_lch_x_kernel(tc, xT, cb, norm, ts, y, wt, offs, out_0, ou
                 in0=planes[t][:].indirect(offsets[:, g * cols:(g + 1) * cols]),
                 in1=norm_row[g][:], op=MULT)
 
-        def weave_pair(h, g, copy):
-            copy(out=kd_in[g][:, :, 2 * h:2 * h + 2], in_=k_f32[h][g][:].rearrange("p e n -> p n e"))
-
-        def quantize_kd(g):
-            nc.vector.quantize_mx(out=kd_codes[g][:].bitcast(E4), scales=kd_scales[g][:],
-                                  in_=kd_in[g][:].rearrange("p n t -> p (n t)"))
+        def weave_k(pair, g):
+            nc.scalar.copy(out=kd_in[g][:, :, 2 * pair:2 * pair + 2], in_=k_f32[pair][g][:].rearrange("p e n -> p n e"))
 
         def turn_k(t, g):
-            bank = bank_tile("k_bank", [P, PACK, P], ("z%d" if t % 2 == 0 else "a%d") % g)
-            src = k_f32[t // 2][g][:, t % 2, :].rearrange("p (s u) -> p u s", u=PACK)
+            turned = bank_tile("turned", [P, PACK, P], (DIFF_BANKS[1:], SUM_BANKS)[t % 2][g])
+            places = k_f32[t // 2][g][:, t % 2, :].rearrange("p (s u) -> p u s", u=PACK)
             for u in range(PACK):
-                nc.tensor.transpose(bank[:, u, :], src[:, u, :], ident[:])
-            nc.scalar.copy(out=kn_in[t // 2][g][:, t % 2, :, :], in_=bank[:].rearrange("s u p -> s p u"))
+                nc.tensor.transpose(turned[:, u, :], places[:, u, :], ident[:])
+            nc.scalar.copy(out=kn_in[t // 2][g][:, t % 2, :, :], in_=turned[:].rearrange("s u p -> s p u"))
 
-        def quantize_kn(h, g):
-            cols = slice(2 * h * P, 2 * (h + 1) * P)
-            nc.vector.quantize_mx(out=kn_codes[g][:, cols].bitcast(E4), scales=kn_scales[g][:, cols],
-                                  in_=kn_in[h][g][:].rearrange("s e p u -> s (e p u)"))
-
-        x_codes = held("x_codes", [P, R], U32)
-        x_scales = held("x_scales", [P, R], U8)
-
-        x_in = held("x_in", [P, PACK, P, PACK], BF16)
-        for t in range(PACK - 1):
+        last = PACK - 1
+        for t in range(last):
             for g in range(G):
                 gather(t, g)
             for g in range(G):
                 turn_k(t, g)
-            if t == 1:
-                nc.vector.tensor_copy(out=x_in[:].rearrange("p j m t -> p m j t"), in_=x_raw[:].rearrange("p t (m j) -> p m j t", j=PACK))
+            if t % 2 == 1:
                 for g in range(G):
-                    quantize_kn(0, g)
-                    weave_pair(0, g, nc.scalar.copy)
-                nc.vector.quantize_mx(out=x_codes[:].bitcast(E4), scales=x_scales[:], in_=x_in[:].rearrange("p j m t -> p (j m t)"))
+                    weave_k(t // 2, g)
 
-        y_dealt = {}
-        deal_tags = ["x_raw", "k_f32_0_0", "k_f32_1_0", "k_f32_1_1"]
+        kn_codes = held("kn_codes", [P, G, D], U32, on="plane2")
+        kn_scales = [held("kn_scales%d" % g, [P, D], U8) for g in range(G)]
 
-        def deal_y(j):
-            dealt = held("y_dealt", [P, G, PACK, P], F32, tag=deal_tags[j])
-            nc.scalar.copy(out=dealt[:].rearrange("p g u s -> p g s u"), in_=y_raw[j][:].rearrange("p (g s u) -> p g s u", g=G, u=PACK))
-            y_dealt[j] = dealt
+        def quantize_kn(pair, g):
+            cols = slice(2 * pair * P, 2 * (pair + 1) * P)
+            nc.vector.quantize_mx(out=kn_codes[:, g, cols].bitcast(E4M3), scales=kn_scales[g][:, cols],
+                                  in_=kn_in[pair][g][:].rearrange("s e p u -> s (e p u)"))
 
-        last = PACK - 1
-        gather(last, 0)
-        gather(last, 1)
-        deal_y(0)
-        weave_pair(1, 0, nc.vector.tensor_copy)
-        weave_pair(1, 1, nc.vector.tensor_copy)
-        quantize_kd(0)
-        quantize_kd(1)
-        order = (0, 1)
-        z_banks, s_banks, neg_a, th, h_in, h_codes, h_scales, accs = {}, {}, {}, {}, {}, {}, {}, {}
+        for g in range(G):
+            quantize_kn(0, g)
+        for g in range(G):
+            gather(last, g)
 
-        def turn_y(j, g):
-            z_banks[j, g] = bank_tile("z_bank", [P, PACK, P], "z%d" % (2 * (j % 2) + g))
-            for u in range(PACK):
-                nc.tensor.matmul(z_banks[j, g][:, u, :], lhsT=y_dealt[j][:, g, u, :], rhs=ident[:], is_transpose=True, start=(u == 0), stop=False)
+        x_in = held("x_in", [P, PACK, P, PACK], BF16)
+        x_codes = held("x_codes", [P, R], U32)
+        x_scales = held("x_scales", [P, R], U8)
+        for half in range(2):
+            nc.vector.tensor_copy(out=x_in[:, :, half * P // 2:(half + 1) * P // 2, :].rearrange("p j m t -> p m j t"),
+                                  in_=x_raw[half][:].rearrange("p t (m j) -> p m j t", j=PACK))
+        for g in range(G):
+            weave_k(last // 2, g)
 
-        def score(j, g):
+        kd_codes, kd_scales = {}, {}
+
+        def quantize_kd(g, on):
+            kd_codes[g] = held("kd_codes%d" % g, [P, PASS], U32, on=on)
+            kd_scales[g] = held("kd_scales%d" % g, [P, PASS], U8)
+            nc.vector.quantize_mx(out=kd_codes[g][:].bitcast(E4M3), scales=kd_scales[g][:],
+                                  in_=kd_in[g][:].rearrange("p n t -> p (n t)"))
+
+        quantize_kd(0, "")
+        nc.vector.quantize_mx(out=x_codes[:].bitcast(E4M3), scales=x_scales[:], in_=x_in[:].rearrange("p j m t -> p (j m t)"))
+        quantize_kd(1, "x_in")
+        for g in range(G):
+            turn_k(last, g)
+
+        y_dealt, scores, neg_a, diff, th, h_in, h_codes, h_scales, sums = {}, {}, {}, {}, {}, {}, {}, {}, {}
+        out_f32 = [held("out_f32_%d" % pair, [P, 2, D], F32) for pair in range(2)]
+        out_in = held("out_in", [P, D, PACK], BF16)
+        out_rows = out_0.rearrange("(m j) d -> m j d", j=PACK)
+        deal_on = {1: "k_f32_0_0", 2: "k_f32_1_0", 3: "k_f32_1_1"}
+
+        def score(i):
+            j, g = divmod(i, G)
             cols = slice(j * P, (j + 1) * P)
-            s_banks[j, g] = bank_tile("s_bank", [P, PASS], "s%d" % g)
-            nc.tensor.matmul_mx(out=s_banks[j, g][:], lhsT=x_codes[:, cols].bitcast(E4), lhsT_scale=x_scales[:, cols],
-                                rhs=kd_codes[g][:].bitcast(E4), rhs_scale=kd_scales[g][:], start=True, stop=True)
+            scores[i] = bank_tile("scores", [P, PASS], SCORE_BANKS[i % len(SCORE_BANKS)])
+            nc.tensor.matmul_mx(out=scores[i][:], lhsT=x_codes[:, cols].bitcast(E4M3), lhsT_scale=x_scales[:, cols],
+                                rhs=kd_codes[g][:].bitcast(E4M3), rhs_scale=kd_scales[g][:], start=True, stop=True)
 
-        def scale_scores(j, g):
-            neg_a[j, g] = ring.tile([P, PACK, P], F32, name="neg_a", align_bytes=64, bufs=4)
-            nc.vector.tensor_tensor(out=neg_a[j, g][:], in0=s_banks[j, g][:].rearrange("p (s u) -> p u s", u=PACK), in1=neg_ts_row[g][:], op=MULT)
+        def scale(i):
+            neg_a[i] = ring.tile([P, PACK, P], F32, name="neg_a", align_bytes=64, bufs=4)
+            nc.vector.tensor_tensor(out=neg_a[i][:], in0=scores[i][:].rearrange("m (s u) -> m u s", u=PACK),
+                                    in1=neg_ts_row[i % G][:], op=MULT)
 
-        def turn_a(j, g):
+        def turn_y(i):
+            j, g = divmod(i, G)
+            if j == 0:
+                places = y_raw[j][:].rearrange("m (g s u) -> m g u s", g=G, u=PACK)
+            else:
+                if g == 0:
+                    y_dealt[j] = held("y_dealt", [P, G, PACK, P], F32, on=deal_on[j])
+                    nc.scalar.copy(out=y_dealt[j][:].rearrange("m g u s -> m g s u"),
+                                   in_=y_raw[j][:].rearrange("m (g s u) -> m g s u", g=G, u=PACK))
+                places = y_dealt[j]
+            diff[i] = bank_tile("diff", [P, PACK, P], DIFF_BANKS[i % len(DIFF_BANKS)])
             for u in range(PACK):
-                nc.tensor.matmul(z_banks[j, g][:, u, :], lhsT=neg_a[j, g][:, u, :], rhs=ident[:], is_transpose=True, start=False, stop=(u == PACK - 1))
+                nc.tensor.matmul(diff[i][:, u, :], lhsT=places[:, g, u, :], rhs=ident[:], is_transpose=True,
+                                 start=(u == 0), stop=False)
 
-        def squash(j, g):
-            if g == order[0]:
+        def turn_a(i):
+            for u in range(PACK):
+                nc.tensor.matmul(diff[i][:, u, :], lhsT=neg_a[i][:, u, :], rhs=ident[:], is_transpose=True,
+                                 start=False, stop=(u == PACK - 1))
+
+        def squash(i):
+            j, g = divmod(i, G)
+            if g == 0:
                 th[j] = ring.tile([P, G, P, PACK], F32, name="th", align_bytes=64)
-            nc.scalar.activation(out=th[j][:, g, :, :], in_=z_banks[j, g][:].rearrange("s u p -> s p u"), func=ACT.Tanh, scale=-1.0)
+            nc.scalar.activation(out=th[j][:, g, :, :], in_=diff[i][:].rearrange("s u m -> s m u"), func=ACT.Tanh, scale=-1.0)
 
-        def weigh(j, gs):
-            if j not in h_in:
+        def weigh(i):
+            j, g = divmod(i, G)
+            if g == 0:
                 h_in[j] = ring.tile([P, G, P, PACK], BF16, name="h_in", align_bytes=64)
-            nc.vector.tensor_tensor(out=h_in[j][:, gs, :, :], in0=th[j][:, gs, :, :], in1=tw[j][:, gs, :, :], op=MULT)
+            nc.vector.tensor_tensor(out=h_in[j][:, g, :, :], in0=th[j][:, g, :, :], in1=tw[j][:, g, :, :], op=MULT)
 
-        def quantize_h(j, gs):
-            if j not in h_codes:
+        def quantize_h(i):
+            j, g = divmod(i, G)
+            if g == 0:
                 h_codes[j] = ring.tile([P, G, P], U32, name="h_codes", align_bytes=64)
                 h_scales[j] = ring.tile([P, G, P], U8, name="h_scales", align_bytes=64)
-            nc.vector.quantize_mx(out=h_codes[j][:, gs, :].rearrange("s g p -> s (g p)").bitcast(E5),
-                                  scales=h_scales[j][:, gs, :].rearrange("s g p -> s (g p)"),
-                                  in_=h_in[j][:, gs, :, :].rearrange("s g p u -> s (g p u)"))
+            nc.vector.quantize_mx(out=h_codes[j][:, g, :].bitcast(E5M2), scales=h_scales[j][:, g, :],
+                                  in_=h_in[j][:, g, :, :].rearrange("s m u -> s (m u)"))
 
-        out_f32 = [held("out_f32_%d" % h, [P, 2, D], F32) for h in range(2)]
-        out_in = held("out_in", [P, D, PACK], BF16)
-        out_rows = out_0.rearrange("(p j) d -> p j d", j=PACK)
-
-        def back(j, g):
-            if g == order[0]:
-                accs[j] = bank_tile("acc", [P, D], "a%d" % (j % 2))
-            nc.tensor.matmul_mx(out=accs[j][:], lhsT=h_codes[j][:, g, :].bitcast(E5), lhsT_scale=h_scales[j][:, g, :],
-                                rhs=kn_codes[g][:].bitcast(E4), rhs_scale=kn_scales[g][:], start=(g == order[0]), stop=(g == order[1]))
-
-        def empty(j, part, parts):
-            width = D // parts
-            nc.scalar.copy(out=out_f32[j // 2][:, j % 2, part * width:(part + 1) * width].rearrange("q (p t) -> q p t", t=PACK),
-                           in_=accs[j][:].rearrange("q (t p) -> q p t", t=PACK)[:, part * width // PACK:(part + 1) * width // PACK, :])
+        def empty(j, cols):
+            nc.scalar.copy(out=out_f32[j // 2][:, j % 2, cols].rearrange("m (p t) -> m p t", t=PACK),
+                           in_=sums[j][:].rearrange("m (t p) -> m p t", t=PACK)[:, cols.start // PACK:cols.stop // PACK, :])
 
         def store(j):
             nc.sync.dma_start(out=out_rows[:, j, :], in_=out_f32[j // 2][:, j % 2, :])
 
-        def weave_out(h, cols):
-            nc.vector.tensor_copy(out=out_in[:, cols, 2 * h:2 * h + 2], in_=out_f32[h][:, :, cols].rearrange("q e d -> q d e"))
+        def back(i):
+            j, g = divmod(i, G)
+            if g == 0:
+                sums[j] = bank_tile("sums", [P, D], SUM_BANKS[j % 2])
+            nc.tensor.matmul_mx(out=sums[j][:], lhsT=h_codes[j][:, g, :].bitcast(E5M2), lhsT_scale=h_scales[j][:, g, :],
+                                rhs=kn_codes[:, g, :].bitcast(E4M3), rhs_scale=kn_scales[g][:],
+                                start=(g == 0), stop=(g == G - 1))
+            if g == G - 1 and j < last:
+                empty(j, slice(0, D))
+                store(j)
 
-        def front(j):
-            for g in order:
-                scale_scores(j, g)
+        def late_kn(i):
+            if i < G:
+                quantize_kn(last // 2, i)
 
-        def middle(j):
-            for g in order:
-                turn_a(j, g)
-                squash(j, g)
+        stages = ((score, SCORE_AHEAD), (turn_a, 0), (scale, SCALE_AHEAD), (squash, 0), (weigh, -WEIGH_BEHIND),
+                  (quantize_h, -QUANT_BEHIND), (late_kn, -1), (back, -BACK_BEHIND), (turn_y, SCORE_AHEAD))
+        for step in range(-SCORE_AHEAD, UNITS + BACK_BEHIND):
+            for stage, distance in stages:
+                if 0 <= step + distance < UNITS:
+                    stage(step + distance)
 
-        def finish(j):
-            for g in order:
-                back(j, g)
-            empty(j, 0, 1)
-            store(j)
+        def weave_out(pair, cols):
+            nc.vector.tensor_copy(out=out_in[:, cols, 2 * pair:2 * pair + 2],
+                                  in_=out_f32[pair][:, :, cols].rearrange("m e d -> m d e"))
 
-        both = slice(0, G)
-        for g in order:
-            turn_y(0, g)
-        deal_y(1)
-        for g in order:
-            score(0, g)
-        for g in order:
-            turn_y(1, g)
-        deal_y(2)
-        for g in order:
-            scale_scores(0, g)
-            score(1, g)
-        middle(0)
-        deal_y(3)
-        for g in order:
-            turn_k(last, g)
-        for g in order:
-            scale_scores(1, g)
-            score(2, g)
-        middle(1)
-        for g in order:
-            turn_y(2, g)
-        weigh(0, both)
-        for g in order:
-            quantize_kn(1, g)
-        for g in order:
-            scale_scores(2, g)
-            score(3, g)
-        quantize_h(0, both)
-        middle(2)
-        finish(0)
-        for g in order:
-            turn_y(3, g)
-        weigh(1, both)
-        front(3)
-        quantize_h(1, both)
-        middle(3)
-        finish(1)
-        weigh(2, both)
-        weigh(3, slice(0, 1))
-        quantize_h(2, both)
-        weigh(3, slice(1, 2))
-        quantize_h(3, slice(0, 1))
-        finish(2)
-        quantize_h(3, slice(1, 2))
-        for g in order:
-            back(3, g)
+        halves = [slice(half * D // 2, (half + 1) * D // 2) for half in range(2)]
         weave_out(0, slice(0, D))
-        for part in range(2):
-            empty(3, part, 2)
-            weave_out(1, slice(part * D // 2, (part + 1) * D // 2))
-        store(3)
+        for cols in halves:
+            empty(last, cols)
+            weave_out(1, cols)
+        store(last)
 
         out_codes = held("out_codes", [P, D], U32)
         out_scales = held("out_scales", [P, D], U8)
-        words = out_1[0].rearrange("p d l -> p (d l)").bitcast(I32)
-        for part in range(2):
-            cols = slice(part * D // 2, (part + 1) * D // 2)
-            nc.vector.quantize_mx(out=out_codes[:, cols].bitcast(E4), scales=out_scales[:, cols], in_=out_in[:, cols, :].rearrange("q d j -> q (d j)"))
+        words = out_1[0].rearrange("m d j -> m (d j)").bitcast(I32)
+        for cols in halves:
+            nc.vector.quantize_mx(out=out_codes[:, cols].bitcast(E4M3), scales=out_scales[:, cols],
+                                  in_=out_in[:, cols, :].rearrange("m d j -> m (d j)"))
             nc.scalar.dma_start(out=words[:, cols], in_=out_codes[:, cols].bitcast(I32))
         for q in range(4):
             queue = nc.scalar if q % 2 else nc.sync

@@ -15,6 +15,7 @@ U8 = mybir.dt.uint8
 E4M3 = mybir.dt.float8_e4m3fn_x4
 E5M2 = mybir.dt.float8_e5m2_x4
 MULT = mybir.AluOpType.mult
+SUBTRACT = mybir.AluOpType.subtract
 ACT = mybir.ActivationFunctionType
 
 P = 128
@@ -22,16 +23,17 @@ PACK = 4
 PASS = P * PACK
 G = N // PASS
 UNITS = PACK * G
+ROW_UNITS = G
+LAST = PACK - 1
 
-SCORE_BANKS = (0, 1, 2)
-DIFF_BANKS = (3, 4, 5)
+SCORE_BANKS = (0, 1)
+DIFF_BANKS = (2, 3, 4, 5)
 SUM_BANKS = (6, 7)
 
-SCORE_AHEAD = 2
-SCALE_AHEAD = 1
-WEIGH_BEHIND = 2
-QUANT_BEHIND = 2
-BACK_BEHIND = 5
+AHEAD = len(SCORE_BANKS)
+WEIGH_BEHIND = 3
+BACK_BEHIND = 7
+KN_BEHIND = 2
 
 
 def tile_attend_gpq_pl_lch_x_kernel(tc, xT, cb, norm, ts, y, wt, offs, out_0, out_1, out_2):
@@ -43,6 +45,9 @@ def tile_attend_gpq_pl_lch_x_kernel(tc, xT, cb, norm, ts, y, wt, offs, out_0, ou
 
         def held(name, shape, dtype, on=""):
             return keep.tile(shape, dtype, name=name, tag=on or name, align_bytes=64)
+
+        def passing(name, shape, dtype, bufs=None):
+            return ring.tile(shape, dtype, name=name, align_bytes=64, bufs=bufs)
 
         def bank_tile(name, shape, bank):
             return psum.tile(shape, F32, name=name, tag="bank%d" % bank)
@@ -72,8 +77,6 @@ def tile_attend_gpq_pl_lch_x_kernel(tc, xT, cb, norm, ts, y, wt, offs, out_0, ou
 
         ident = held("ident", [P, P], F32)
         make_identity(nc, ident[:])
-        warm = held("warm", [P, 8], F32)
-        nc.scalar.activation(out=warm[:], in_=ident[:, 0:8], func=ACT.Tanh)
 
         def spread(columns, bank):
             rows = bank_tile("rows", [P, PACK, P], bank)
@@ -81,53 +84,58 @@ def tile_attend_gpq_pl_lch_x_kernel(tc, xT, cb, norm, ts, y, wt, offs, out_0, ou
                 nc.tensor.transpose(rows[:, u, :], columns[:, u:u + 1].to_broadcast([P, P]), ident[:])
             return rows
 
+        def in_column_order(tile):
+            return tile[:].rearrange("q (s u) -> q s u", u=PACK)
+
         norm_row = [held("norm_row%d" % g, [P, PASS], F32) for g in range(G)]
-        neg_ts_row = [held("neg_ts_row%d" % g, [P, PACK, P], F32) for g in range(G)]
-        tw = [held("tw%d" % j, [P, G, P, PACK], F32) for j in range(PACK)]
+        ts_row = [held("ts_row%d" % g, [P, PASS], F32) for g in range(G)]
+        neg_ts_places = [held("neg_ts_places%d" % g, [P, PACK, P], F32) for g in range(G)]
         for g in range(G):
             rows = spread(norm_col[:, g, :], SCORE_BANKS[g])
-            nc.scalar.copy(out=norm_row[g][:].rearrange("q (s u) -> q s u", u=PACK), in_=rows[:].rearrange("q u s -> q s u"))
-        wt_rows = spread(wt_col, SCORE_BANKS[2])
-        for j in range(PACK):
+            nc.scalar.copy(out=in_column_order(norm_row[g]), in_=rows[:].rearrange("q u s -> q s u"))
+        wt_rows = spread(wt_col, DIFF_BANKS[0])
+        ts_wt = {}
+        for j in range(ROW_UNITS // G, PACK):
+            ts_wt[j] = held("ts_wt%d" % j, [P, G, P, PACK], F32)
             nc.vector.tensor_tensor(
-                out=tw[j][:],
+                out=ts_wt[j][:],
                 in0=wt_rows[:, j, :].unsqueeze(1).unsqueeze(3).to_broadcast([P, G, P, PACK]),
                 in1=ts_col[:].unsqueeze(2).to_broadcast([P, G, P, PACK]),
                 op=MULT)
         for g in range(G):
-            rows = spread(ts_col[:, g, :], DIFF_BANKS[g])
-            nc.scalar.activation(out=neg_ts_row[g][:], in_=rows[:], func=ACT.Copy, scale=-1.0)
+            rows = spread(ts_col[:, g, :], DIFF_BANKS[1 + g])
+            nc.scalar.activation(out=neg_ts_places[g][:], in_=rows[:], func=ACT.Copy, scale=-1.0)
+            nc.scalar.copy(out=in_column_order(ts_row[g]), in_=rows[:].rearrange("q u s -> q s u"))
 
         k_f32 = [[held("k_f32_%d_%d" % (pair, g), [P, 2, PASS], F32) for g in range(G)] for pair in range(2)]
         kd_in = [held("kd_in%d" % g, [P, PASS, PACK], BF16) for g in range(G)]
         kn_in = [[held("kn_in_%d_%d" % (pair, g), [P, 2, P, PACK], BF16) for g in range(G)] for pair in range(2)]
 
         def gather(t, g):
-            cols = PASS // 16
+            list_cols = PASS // 16
             nc.vector.tensor_tensor(
                 out=k_f32[t // 2][g][:, t % 2, :],
-                in0=planes[t][:].indirect(offsets[:, g * cols:(g + 1) * cols]),
+                in0=planes[t][:].indirect(offsets[:, g * list_cols:(g + 1) * list_cols]),
                 in1=norm_row[g][:], op=MULT)
 
-        def weave_k(pair, g):
-            nc.scalar.copy(out=kd_in[g][:, :, 2 * pair:2 * pair + 2], in_=k_f32[pair][g][:].rearrange("p e n -> p n e"))
+        def weave_k(pair, g, copy):
+            copy(out=kd_in[g][:, :, 2 * pair:2 * pair + 2], in_=k_f32[pair][g][:].rearrange("p e n -> p n e"))
 
         def turn_k(t, g):
-            turned = bank_tile("turned", [P, PACK, P], (DIFF_BANKS[1:], SUM_BANKS)[t % 2][g])
+            turned = bank_tile("turned_k", [P, PACK, P], (DIFF_BANKS[2:], SUM_BANKS)[t % 2][g])
             places = k_f32[t // 2][g][:, t % 2, :].rearrange("p (s u) -> p u s", u=PACK)
             for u in range(PACK):
                 nc.tensor.transpose(turned[:, u, :], places[:, u, :], ident[:])
             nc.scalar.copy(out=kn_in[t // 2][g][:, t % 2, :, :], in_=turned[:].rearrange("s u p -> s p u"))
 
-        last = PACK - 1
-        for t in range(last):
+        for t in range(LAST):
             for g in range(G):
                 gather(t, g)
             for g in range(G):
                 turn_k(t, g)
             if t % 2 == 1:
                 for g in range(G):
-                    weave_k(t // 2, g)
+                    weave_k(t // 2, g, nc.scalar.copy)
 
         kn_codes = held("kn_codes", [P, G, D], U32, on="plane2")
         kn_scales = [held("kn_scales%d" % g, [P, D], U8) for g in range(G)]
@@ -140,36 +148,37 @@ def tile_attend_gpq_pl_lch_x_kernel(tc, xT, cb, norm, ts, y, wt, offs, out_0, ou
         for g in range(G):
             quantize_kn(0, g)
         for g in range(G):
-            gather(last, g)
+            gather(LAST, g)
 
         x_in = held("x_in", [P, PACK, P, PACK], BF16)
         x_codes = held("x_codes", [P, R], U32)
         x_scales = held("x_scales", [P, R], U8)
-        for half in range(2):
-            nc.vector.tensor_copy(out=x_in[:, :, half * P // 2:(half + 1) * P // 2, :].rearrange("p j m t -> p m j t"),
-                                  in_=x_raw[half][:].rearrange("p t (m j) -> p m j t", j=PACK))
-        for g in range(G):
-            weave_k(last // 2, g)
+        for half, copy in enumerate((nc.scalar.copy, nc.vector.tensor_copy)):
+            copy(out=x_in[:, :, half * P // 2:(half + 1) * P // 2, :].rearrange("p j m t -> p m j t"),
+                 in_=x_raw[half][:].rearrange("p t (m j) -> p m j t", j=PACK))
+        for g, copy in enumerate((nc.vector.tensor_copy, nc.scalar.copy)):
+            weave_k(LAST // 2, g, copy)
 
-        kd_codes, kd_scales = {}, {}
+        kd_codes = [held("kd_codes0", [P, PASS], U32, on="x_raw0"), held("kd_codes1", [P, PASS], U32)]
+        kd_scales = [held("kd_scales%d" % g, [P, PASS], U8) for g in range(G)]
 
-        def quantize_kd(g, on):
-            kd_codes[g] = held("kd_codes%d" % g, [P, PASS], U32, on=on)
-            kd_scales[g] = held("kd_scales%d" % g, [P, PASS], U8)
+        def quantize_kd(g):
             nc.vector.quantize_mx(out=kd_codes[g][:].bitcast(E4M3), scales=kd_scales[g][:],
                                   in_=kd_in[g][:].rearrange("p n t -> p (n t)"))
 
-        quantize_kd(0, "")
+        quantize_kd(0)
         nc.vector.quantize_mx(out=x_codes[:].bitcast(E4M3), scales=x_scales[:], in_=x_in[:].rearrange("p j m t -> p (j m t)"))
-        quantize_kd(1, "x_in")
+        quantize_kd(1)
         for g in range(G):
-            turn_k(last, g)
+            turn_k(LAST, g)
 
-        y_dealt, scores, neg_a, diff, th, h_in, h_codes, h_scales, sums = {}, {}, {}, {}, {}, {}, {}, {}, {}
+        scores, scaled, y_places, diff, tanh, h_in, h_codes, h_scales, sums = {}, {}, {}, {}, {}, {}, {}, {}, {}
         out_f32 = [held("out_f32_%d" % pair, [P, 2, D], F32) for pair in range(2)]
-        out_in = held("out_in", [P, D, PACK], BF16)
         out_rows = out_0.rearrange("(m j) d -> m j d", j=PACK)
-        deal_on = {1: "k_f32_0_0", 2: "k_f32_1_0", 3: "k_f32_1_1"}
+
+        def y_half(i):
+            j, g = divmod(i, G)
+            return y_raw[j][:, g * PASS:(g + 1) * PASS]
 
         def score(i):
             j, g = divmod(i, G)
@@ -179,49 +188,74 @@ def tile_attend_gpq_pl_lch_x_kernel(tc, xT, cb, norm, ts, y, wt, offs, out_0, ou
                                 rhs=kd_codes[g][:].bitcast(E4M3), rhs_scale=kd_scales[g][:], start=True, stop=True)
 
         def scale(i):
-            neg_a[i] = ring.tile([P, PACK, P], F32, name="neg_a", align_bytes=64, bufs=4)
-            nc.vector.tensor_tensor(out=neg_a[i][:], in0=scores[i][:].rearrange("m (s u) -> m u s", u=PACK),
-                                    in1=neg_ts_row[i % G][:], op=MULT)
+            if i < ROW_UNITS:
+                scaled[i] = passing("a_rows", [P, PASS], F32)
+                nc.vector.tensor_tensor(out=scaled[i][:], in0=scores[i][:], in1=ts_row[i % G][:], op=MULT)
+            else:
+                scaled[i] = passing("neg_a", [P, PACK, P], F32)
+                nc.vector.tensor_tensor(out=scaled[i][:], in0=scores[i][:].rearrange("m (s u) -> m u s", u=PACK),
+                                        in1=neg_ts_places[i % G][:], op=MULT)
+
+        def deal_y(i):
+            if i >= ROW_UNITS:
+                y_places[i] = passing("y_places", [P, PACK, P], F32, bufs=4)
+                nc.scalar.copy(out=y_places[i][:].rearrange("m u s -> m s u"), in_=y_half(i).rearrange("m (s u) -> m s u", u=PACK))
 
         def turn_y(i):
-            j, g = divmod(i, G)
-            if j == 0:
-                places = y_raw[j][:].rearrange("m (g s u) -> m g u s", g=G, u=PACK)
-            else:
-                if g == 0:
-                    y_dealt[j] = held("y_dealt", [P, G, PACK, P], F32, on=deal_on[j])
-                    nc.scalar.copy(out=y_dealt[j][:].rearrange("m g u s -> m g s u"),
-                                   in_=y_raw[j][:].rearrange("m (g s u) -> m g s u", g=G, u=PACK))
-                places = y_dealt[j]
-            diff[i] = bank_tile("diff", [P, PACK, P], DIFF_BANKS[i % len(DIFF_BANKS)])
-            for u in range(PACK):
-                nc.tensor.matmul(diff[i][:, u, :], lhsT=places[:, g, u, :], rhs=ident[:], is_transpose=True,
-                                 start=(u == 0), stop=False)
+            if i >= ROW_UNITS:
+                diff[i] = bank_tile("diff", [P, PACK, P], DIFF_BANKS[i % len(DIFF_BANKS)])
+                for u in range(PACK):
+                    nc.tensor.matmul(diff[i][:, u, :], lhsT=y_places[i][:, u, :], rhs=ident[:], is_transpose=True,
+                                     start=(u == 0), stop=False)
 
-        def turn_a(i):
-            for u in range(PACK):
-                nc.tensor.matmul(diff[i][:, u, :], lhsT=neg_a[i][:, u, :], rhs=ident[:], is_transpose=True,
-                                 start=False, stop=(u == PACK - 1))
+        def subtract(i):
+            if i < ROW_UNITS:
+                diff[i] = passing("z_rows", [P, PASS], F32)
+                nc.vector.tensor_tensor(out=diff[i][:], in0=scaled[i][:], in1=y_half(i), op=SUBTRACT)
+            else:
+                for u in range(PACK):
+                    nc.tensor.matmul(diff[i][:, u, :], lhsT=scaled[i][:, u, :], rhs=ident[:], is_transpose=True,
+                                     start=False, stop=(u == PACK - 1))
 
         def squash(i):
             j, g = divmod(i, G)
-            if g == 0:
-                th[j] = ring.tile([P, G, P, PACK], F32, name="th", align_bytes=64)
-            nc.scalar.activation(out=th[j][:, g, :, :], in_=diff[i][:].rearrange("s u m -> s m u"), func=ACT.Tanh, scale=-1.0)
+            if i < ROW_UNITS:
+                tanh[i] = passing("tanh_rows", [P, PASS], F32)
+                nc.scalar.activation(out=tanh[i][:], in_=diff[i][:], func=ACT.Tanh)
+            else:
+                if g == 0:
+                    tanh[i] = tanh[i + 1] = passing("tanh_woven", [P, G, P, PACK], F32)
+                nc.scalar.activation(out=tanh[i][:, g, :, :], in_=diff[i][:].rearrange("s u m -> s m u"),
+                                     func=ACT.Tanh, scale=-1.0)
 
         def weigh(i):
             j, g = divmod(i, G)
             if g == 0:
-                h_in[j] = ring.tile([P, G, P, PACK], BF16, name="h_in", align_bytes=64)
-            nc.vector.tensor_tensor(out=h_in[j][:, g, :, :], in0=th[j][:, g, :, :], in1=tw[j][:, g, :, :], op=MULT)
+                h_in[j] = passing("h_in", [P, G, P, PACK], BF16)
+            if i < ROW_UNITS:
+                h_rows = passing("h_rows", [P, PASS], BF16)
+                nc.vector.scalar_tensor_tensor(out=h_rows[:], in0=tanh[i][:], scalar=wt_col[:, j:j + 1], in1=ts_row[g][:],
+                                               op0=MULT, op1=MULT)
+                pairs = h_rows[:].bitcast(F32).rearrange("m (s v) -> m v s", v=2)
+                turned = bank_tile("turned_h", [P, 2, P], SUM_BANKS[1 - g])
+                for v in range(2):
+                    nc.tensor.transpose(turned[:, v, :], pairs[:, v, :], ident[:])
+                woven = h_in[j][:, g, :, :].rearrange("s m u -> s (m u)").bitcast(F32)
+                nc.scalar.copy(out=woven.rearrange("s (m v) -> s m v", v=2), in_=turned[:].rearrange("s v m -> s m v"))
+            else:
+                nc.vector.tensor_tensor(out=h_in[j][:, g, :, :], in0=tanh[i][:, g, :, :], in1=ts_wt[j][:, g, :, :], op=MULT)
 
         def quantize_h(i):
             j, g = divmod(i, G)
             if g == 0:
-                h_codes[j] = ring.tile([P, G, P], U32, name="h_codes", align_bytes=64)
-                h_scales[j] = ring.tile([P, G, P], U8, name="h_scales", align_bytes=64)
+                h_codes[j] = passing("h_codes", [P, G, P], U32)
+                h_scales[j] = passing("h_scales", [P, G, P], U8)
             nc.vector.quantize_mx(out=h_codes[j][:, g, :].bitcast(E5M2), scales=h_scales[j][:, g, :],
                                   in_=h_in[j][:, g, :, :].rearrange("s m u -> s (m u)"))
+
+        def quantize_late_kn(g):
+            if g < G:
+                quantize_kn(LAST // 2, g)
 
         def empty(j, cols):
             nc.scalar.copy(out=out_f32[j // 2][:, j % 2, cols].rearrange("m (p t) -> m p t", t=PACK),
@@ -233,38 +267,37 @@ def tile_attend_gpq_pl_lch_x_kernel(tc, xT, cb, norm, ts, y, wt, offs, out_0, ou
         def back(i):
             j, g = divmod(i, G)
             if g == 0:
-                sums[j] = bank_tile("sums", [P, D], SUM_BANKS[j % 2])
+                sums[j] = bank_tile("sums", [P, D], SUM_BANKS[j % len(SUM_BANKS)])
             nc.tensor.matmul_mx(out=sums[j][:], lhsT=h_codes[j][:, g, :].bitcast(E5M2), lhsT_scale=h_scales[j][:, g, :],
                                 rhs=kn_codes[:, g, :].bitcast(E4M3), rhs_scale=kn_scales[g][:],
                                 start=(g == 0), stop=(g == G - 1))
-            if g == G - 1 and j < last:
+            if g == G - 1 and j < LAST:
                 empty(j, slice(0, D))
                 store(j)
 
-        def late_kn(i):
-            if i < G:
-                quantize_kn(last // 2, i)
-
-        stages = ((score, SCORE_AHEAD), (turn_a, 0), (scale, SCALE_AHEAD), (squash, 0), (weigh, -WEIGH_BEHIND),
-                  (quantize_h, -QUANT_BEHIND), (late_kn, -1), (back, -BACK_BEHIND), (turn_y, SCORE_AHEAD))
-        for step in range(-SCORE_AHEAD, UNITS + BACK_BEHIND):
+        stages = ((score, AHEAD), (subtract, 0), (scale, 1), (squash, 0), (weigh, -WEIGH_BEHIND),
+                  (quantize_h, -WEIGH_BEHIND - 1), (quantize_late_kn, -KN_BEHIND), (back, -BACK_BEHIND),
+                  (deal_y, AHEAD + 1), (turn_y, AHEAD))
+        for step in range(-AHEAD - 1, UNITS + BACK_BEHIND):
             for stage, distance in stages:
                 if 0 <= step + distance < UNITS:
                     stage(step + distance)
+
+        out_in = held("out_in", [P, D, PACK], BF16)
+        out_codes = held("out_codes", [P, D], U32)
+        out_scales = held("out_scales", [P, D], U8)
+        halves = [slice(half * D // 2, (half + 1) * D // 2) for half in range(2)]
 
         def weave_out(pair, cols):
             nc.vector.tensor_copy(out=out_in[:, cols, 2 * pair:2 * pair + 2],
                                   in_=out_f32[pair][:, :, cols].rearrange("m e d -> m d e"))
 
-        halves = [slice(half * D // 2, (half + 1) * D // 2) for half in range(2)]
         weave_out(0, slice(0, D))
         for cols in halves:
-            empty(last, cols)
-            weave_out(1, cols)
-        store(last)
+            empty(LAST, cols)
+            weave_out(LAST // 2, cols)
+        store(LAST)
 
-        out_codes = held("out_codes", [P, D], U32)
-        out_scales = held("out_scales", [P, D], U8)
         words = out_1[0].rearrange("m d j -> m (d j)").bitcast(I32)
         for cols in halves:
             nc.vector.quantize_mx(out=out_codes[:, cols].bitcast(E4M3), scales=out_scales[:, cols],

@@ -32,6 +32,7 @@ SUM_BANKS = (6, 7)
 
 AHEAD = len(SCORE_BANKS)
 WEIGH_BEHIND = 3
+QUANTIZE_BEHIND = 5
 BACK_BEHIND = 7
 KN_BEHIND = 2
 
@@ -267,7 +268,7 @@ def tile_attend_gpq_pl_lch_x_kernel(tc, xT, cb, norm, ts, y, wt, offs, out_0, ou
         def back(i):
             j, g = divmod(i, G)
             if g == 0:
-                sums[j] = bank_tile("sums", [P, D], SUM_BANKS[j % len(SUM_BANKS)])
+                sums[j] = bank_tile("sums", [P, D], (SUM_BANKS + SCORE_BANKS)[j])
             nc.tensor.matmul_mx(out=sums[j][:], lhsT=h_codes[j][:, g, :].bitcast(E5M2), lhsT_scale=h_scales[j][:, g, :],
                                 rhs=kn_codes[:, g, :].bitcast(E4M3), rhs_scale=kn_scales[g][:],
                                 start=(g == 0), stop=(g == G - 1))
@@ -276,7 +277,7 @@ def tile_attend_gpq_pl_lch_x_kernel(tc, xT, cb, norm, ts, y, wt, offs, out_0, ou
                 store(j)
 
         stages = ((score, AHEAD), (subtract, 0), (scale, 1), (squash, 0), (weigh, -WEIGH_BEHIND),
-                  (quantize_h, -WEIGH_BEHIND - 1), (quantize_late_kn, -KN_BEHIND), (back, -BACK_BEHIND),
+                  (quantize_h, -QUANTIZE_BEHIND), (quantize_late_kn, -KN_BEHIND), (back, -BACK_BEHIND),
                   (deal_y, AHEAD + 1), (turn_y, AHEAD))
         for step in range(-AHEAD - 1, UNITS + BACK_BEHIND):
             for stage, distance in stages:

@@ -64,11 +64,11 @@ def tile_attend_gpq_pl_lch_x_kernel(tc, xT, cb, norm, ts, y, wt, offs, out_0, ou
         x_rows = xT.rearrange("(p t) r -> p t r", t=PACK)
         y_rows = y.rearrange("(m j) n -> m j n", j=PACK)
 
-        nc.sync.dma_start(out=wt_col[:], in_=wt.rearrange("(m j) o -> m (j o)", j=PACK))
-        nc.sync.dma_start(out=ts_col[:], in_=ts[0, :].rearrange("(g s u) -> s g u", g=G, u=PACK))
         nc.sync.dma_start(out=norm_col[:], in_=norm[0, :].rearrange("(g s u) -> s g u", g=G, u=PACK))
         nc.sync.dma_start(out=planes[0][:], in_=cb_rows[:, 0, :])
         nc.sync.dma_start(offsets[:], offs)
+        nc.sync.dma_start(out=wt_col[:], in_=wt.rearrange("(m j) o -> m (j o)", j=PACK))
+        nc.sync.dma_start(out=ts_col[:], in_=ts[0, :].rearrange("(g s u) -> s g u", g=G, u=PACK))
         for t in range(1, PACK):
             nc.sync.dma_start(out=planes[t][:], in_=cb_rows[:, t, :])
         for half in range(2):
@@ -155,8 +155,8 @@ def tile_attend_gpq_pl_lch_x_kernel(tc, xT, cb, norm, ts, y, wt, offs, out_0, ou
         x_codes = held("x_codes", [P, R], U32)
         x_scales = held("x_scales", [P, R], U8)
         for half, copy in enumerate((nc.scalar.copy, nc.vector.tensor_copy)):
-            copy(out=x_in[:, :, half * P // 2:(half + 1) * P // 2, :].rearrange("p j m t -> p m j t"),
-                 in_=x_raw[half][:].rearrange("p t (m j) -> p m j t", j=PACK))
+            copy(out=x_in[:, :, half * P // 2:(half + 1) * P // 2, :].rearrange("p j m t -> p m t j"),
+                 in_=x_raw[half][:].rearrange("p t (m j) -> p m t j", j=PACK))
         for g, copy in enumerate((nc.vector.tensor_copy, nc.scalar.copy)):
             weave_k(LAST // 2, g, copy)
 
@@ -289,14 +289,16 @@ def tile_attend_gpq_pl_lch_x_kernel(tc, xT, cb, norm, ts, y, wt, offs, out_0, ou
         out_scales = held("out_scales", [P, D], U8)
         halves = [slice(half * D // 2, (half + 1) * D // 2) for half in range(2)]
 
-        def weave_out(pair, cols):
-            nc.vector.tensor_copy(out=out_in[:, cols, 2 * pair:2 * pair + 2],
-                                  in_=out_f32[pair][:, :, cols].rearrange("m e d -> m d e"))
+        def weave_out(pair, cols, copy=nc.vector.tensor_copy):
+            copy(out=out_in[:, cols, 2 * pair:2 * pair + 2], in_=out_f32[pair][:, :, cols].rearrange("m e d -> m d e"))
 
         weave_out(0, slice(0, D))
-        for cols in halves:
+        fourths = [slice(q * D // 4, (q + 1) * D // 4) for q in range(4)]
+        for cols in fourths:
             empty(LAST, cols)
+        for cols in fourths[:LAST]:
             weave_out(LAST // 2, cols)
+        weave_out(LAST // 2, fourths[LAST], nc.scalar.copy)
         store(LAST)
 
         words = out_1[0].rearrange("m d j -> m (d j)").bitcast(I32)

@@ -22,26 +22,27 @@ P = 128
 PACK = 4
 PASS = P * PACK
 G = N // PASS
-UNITS = PACK * G
-ROW_UNITS = G
+UNITS = ((0, 0), (1, 0), (0, 1), (1, 1)) + tuple((j, g) for j in range(2, PACK) for g in range(G))
+ROW_UNITS = 2
+SUM_UNITS = len(UNITS) - ROW_UNITS
 LAST = PACK - 1
 
-SCORE_BANKS = (0, 1)
-DIFF_BANKS = (2, 3, 4, 5)
+SCORE_BANKS = (0, 1, 2)
+DIFF_BANKS = (3, 4, 5)
 SUM_BANKS = (6, 7)
 
-AHEAD = len(SCORE_BANKS)
+SCORE_AHEAD = len(SCORE_BANKS)
+DEAL_AHEAD = SCORE_AHEAD + 1
 WEIGH_BEHIND = 3
 QUANTIZE_BEHIND = 5
 BACK_BEHIND = 7
-KN_BEHIND = 2
 
 
 def tile_attend_gpq_pl_lch_x_kernel(tc, xT, cb, norm, ts, y, wt, offs, out_0, out_1, out_2):
     nc = tc.nc
     with ExitStack() as ctx:
         keep = ctx.enter_context(tc.tile_pool(name="keep", bufs=1))
-        ring = ctx.enter_context(tc.tile_pool(name="ring", bufs=3))
+        ring = ctx.enter_context(tc.tile_pool(name="ring", bufs=ROW_UNITS))
         psum = ctx.enter_context(tc.psum_pool(name="psum", bufs=1))
 
         def held(name, shape, dtype, on=""):
@@ -64,11 +65,11 @@ def tile_attend_gpq_pl_lch_x_kernel(tc, xT, cb, norm, ts, y, wt, offs, out_0, ou
         x_rows = xT.rearrange("(p t) r -> p t r", t=PACK)
         y_rows = y.rearrange("(m j) n -> m j n", j=PACK)
 
+        nc.sync.dma_start(out=wt_col[:], in_=wt.rearrange("(m j) o -> m (j o)", j=PACK))
+        nc.sync.dma_start(out=ts_col[:], in_=ts[0, :].rearrange("(g s u) -> s g u", g=G, u=PACK))
         nc.sync.dma_start(out=norm_col[:], in_=norm[0, :].rearrange("(g s u) -> s g u", g=G, u=PACK))
         nc.sync.dma_start(out=planes[0][:], in_=cb_rows[:, 0, :])
         nc.sync.dma_start(offsets[:], offs)
-        nc.sync.dma_start(out=wt_col[:], in_=wt.rearrange("(m j) o -> m (j o)", j=PACK))
-        nc.sync.dma_start(out=ts_col[:], in_=ts[0, :].rearrange("(g s u) -> s g u", g=G, u=PACK))
         for t in range(1, PACK):
             nc.sync.dma_start(out=planes[t][:], in_=cb_rows[:, t, :])
         for half in range(2):
@@ -89,24 +90,23 @@ def tile_attend_gpq_pl_lch_x_kernel(tc, xT, cb, norm, ts, y, wt, offs, out_0, ou
             return tile[:].rearrange("q (s u) -> q s u", u=PACK)
 
         norm_row = [held("norm_row%d" % g, [P, PASS], F32) for g in range(G)]
-        ts_row = [held("ts_row%d" % g, [P, PASS], F32) for g in range(G)]
+        ts_row = held("ts_row", [P, PASS], F32)
         neg_ts_places = [held("neg_ts_places%d" % g, [P, PACK, P], F32) for g in range(G)]
         for g in range(G):
             rows = spread(norm_col[:, g, :], SCORE_BANKS[g])
             nc.scalar.copy(out=in_column_order(norm_row[g]), in_=rows[:].rearrange("q u s -> q s u"))
         wt_rows = spread(wt_col, DIFF_BANKS[0])
         ts_wt = {}
-        for j in range(ROW_UNITS // G, PACK):
-            ts_wt[j] = held("ts_wt%d" % j, [P, G, P, PACK], F32)
-            nc.vector.tensor_tensor(
-                out=ts_wt[j][:],
-                in0=wt_rows[:, j, :].unsqueeze(1).unsqueeze(3).to_broadcast([P, G, P, PACK]),
-                in1=ts_col[:].unsqueeze(2).to_broadcast([P, G, P, PACK]),
-                op=MULT)
+        for i in range(ROW_UNITS, len(UNITS)):
+            j, g = UNITS[i]
+            ts_wt[i] = held("ts_wt%d" % i, [P, P, PACK], F32)
+            nc.vector.tensor_tensor(out=ts_wt[i][:], in0=wt_rows[:, j, :].unsqueeze(2).to_broadcast([P, P, PACK]),
+                                    in1=ts_col[:, g, :].unsqueeze(1).to_broadcast([P, P, PACK]), op=MULT)
         for g in range(G):
-            rows = spread(ts_col[:, g, :], DIFF_BANKS[1 + g])
+            rows = spread(ts_col[:, g, :], SUM_BANKS[g])
             nc.scalar.activation(out=neg_ts_places[g][:], in_=rows[:], func=ACT.Copy, scale=-1.0)
-            nc.scalar.copy(out=in_column_order(ts_row[g]), in_=rows[:].rearrange("q u s -> q s u"))
+            if g == 0:
+                nc.scalar.copy(out=in_column_order(ts_row), in_=rows[:].rearrange("q u s -> q s u"))
 
         k_f32 = [[held("k_f32_%d_%d" % (pair, g), [P, 2, PASS], F32) for g in range(G)] for pair in range(2)]
         kd_in = [held("kd_in%d" % g, [P, PASS, PACK], BF16) for g in range(G)]
@@ -123,7 +123,7 @@ def tile_attend_gpq_pl_lch_x_kernel(tc, xT, cb, norm, ts, y, wt, offs, out_0, ou
             copy(out=kd_in[g][:, :, 2 * pair:2 * pair + 2], in_=k_f32[pair][g][:].rearrange("p e n -> p n e"))
 
         def turn_k(t, g):
-            turned = bank_tile("turned_k", [P, PACK, P], (DIFF_BANKS[2:], SUM_BANKS)[t % 2][g])
+            turned = bank_tile("turned_k", [P, PACK, P], (DIFF_BANKS[1:], SUM_BANKS)[t % 2][g])
             places = k_f32[t // 2][g][:, t % 2, :].rearrange("p (s u) -> p u s", u=PACK)
             for u in range(PACK):
                 nc.tensor.transpose(turned[:, u, :], places[:, u, :], ident[:])
@@ -168,21 +168,26 @@ def tile_attend_gpq_pl_lch_x_kernel(tc, xT, cb, norm, ts, y, wt, offs, out_0, ou
                                   in_=kd_in[g][:].rearrange("p n t -> p (n t)"))
 
         quantize_kd(0)
-        nc.vector.quantize_mx(out=x_codes[:].bitcast(E4M3), scales=x_scales[:], in_=x_in[:].rearrange("p j m t -> p (j m t)"))
+        for pair in range(2):
+            cols = slice(2 * pair * P, 2 * (pair + 1) * P)
+            nc.vector.quantize_mx(out=x_codes[:, cols].bitcast(E4M3), scales=x_scales[:, cols],
+                                  in_=x_in[:, 2 * pair:2 * pair + 2, :, :].rearrange("p j m t -> p (j m t)"))
         quantize_kd(1)
         for g in range(G):
             turn_k(LAST, g)
+        for g in range(G):
+            quantize_kn(LAST // 2, g)
 
         scores, scaled, y_places, diff, tanh, h_in, h_codes, h_scales, sums = {}, {}, {}, {}, {}, {}, {}, {}, {}
         out_f32 = [held("out_f32_%d" % pair, [P, 2, D], F32) for pair in range(2)]
         out_rows = out_0.rearrange("(m j) d -> m j d", j=PACK)
 
         def y_half(i):
-            j, g = divmod(i, G)
+            j, g = UNITS[i]
             return y_raw[j][:, g * PASS:(g + 1) * PASS]
 
         def score(i):
-            j, g = divmod(i, G)
+            j, g = UNITS[i]
             cols = slice(j * P, (j + 1) * P)
             scores[i] = bank_tile("scores", [P, PASS], SCORE_BANKS[i % len(SCORE_BANKS)])
             nc.tensor.matmul_mx(out=scores[i][:], lhsT=x_codes[:, cols].bitcast(E4M3), lhsT_scale=x_scales[:, cols],
@@ -191,15 +196,15 @@ def tile_attend_gpq_pl_lch_x_kernel(tc, xT, cb, norm, ts, y, wt, offs, out_0, ou
         def scale(i):
             if i < ROW_UNITS:
                 scaled[i] = passing("a_rows", [P, PASS], F32)
-                nc.vector.tensor_tensor(out=scaled[i][:], in0=scores[i][:], in1=ts_row[i % G][:], op=MULT)
+                nc.vector.tensor_tensor(out=scaled[i][:], in0=scores[i][:], in1=ts_row[:], op=MULT)
             else:
-                scaled[i] = passing("neg_a", [P, PACK, P], F32)
+                scaled[i] = passing("neg_a", [P, PACK, P], F32, bufs=SUM_UNITS)
                 nc.vector.tensor_tensor(out=scaled[i][:], in0=scores[i][:].rearrange("m (s u) -> m u s", u=PACK),
-                                        in1=neg_ts_places[i % G][:], op=MULT)
+                                        in1=neg_ts_places[UNITS[i][1]][:], op=MULT)
 
         def deal_y(i):
             if i >= ROW_UNITS:
-                y_places[i] = passing("y_places", [P, PACK, P], F32, bufs=4)
+                y_places[i] = passing("y_places", [P, PACK, P], F32, bufs=SUM_UNITS)
                 nc.scalar.copy(out=y_places[i][:].rearrange("m u s -> m s u"), in_=y_half(i).rearrange("m (s u) -> m s u", u=PACK))
 
         def turn_y(i):
@@ -219,44 +224,34 @@ def tile_attend_gpq_pl_lch_x_kernel(tc, xT, cb, norm, ts, y, wt, offs, out_0, ou
                                      start=False, stop=(u == PACK - 1))
 
         def squash(i):
-            j, g = divmod(i, G)
             if i < ROW_UNITS:
                 tanh[i] = passing("tanh_rows", [P, PASS], F32)
                 nc.scalar.activation(out=tanh[i][:], in_=diff[i][:], func=ACT.Tanh)
             else:
-                if g == 0:
-                    tanh[i] = tanh[i + 1] = passing("tanh_woven", [P, G, P, PACK], F32)
-                nc.scalar.activation(out=tanh[i][:, g, :, :], in_=diff[i][:].rearrange("s u m -> s m u"),
-                                     func=ACT.Tanh, scale=-1.0)
+                tanh[i] = passing("tanh_woven", [P, P, PACK], F32, bufs=SUM_UNITS)
+                nc.scalar.activation(out=tanh[i][:], in_=diff[i][:].rearrange("s u m -> s m u"), func=ACT.Tanh, scale=-1.0)
 
         def weigh(i):
-            j, g = divmod(i, G)
-            if g == 0:
-                h_in[j] = passing("h_in", [P, G, P, PACK], BF16)
+            j, g = UNITS[i]
+            h_in[i] = passing("h_in", [P, P, PACK], BF16, bufs=len(UNITS))
             if i < ROW_UNITS:
                 h_rows = passing("h_rows", [P, PASS], BF16)
-                nc.vector.scalar_tensor_tensor(out=h_rows[:], in0=tanh[i][:], scalar=wt_col[:, j:j + 1], in1=ts_row[g][:],
+                nc.vector.scalar_tensor_tensor(out=h_rows[:], in0=tanh[i][:], scalar=wt_col[:, j:j + 1], in1=ts_row[:],
                                                op0=MULT, op1=MULT)
                 pairs = h_rows[:].bitcast(F32).rearrange("m (s v) -> m v s", v=2)
-                turned = bank_tile("turned_h", [P, 2, P], SUM_BANKS[1 - g])
+                turned = bank_tile("turned_h", [P, 2, P], SUM_BANKS[1])
                 for v in range(2):
                     nc.tensor.transpose(turned[:, v, :], pairs[:, v, :], ident[:])
-                woven = h_in[j][:, g, :, :].rearrange("s m u -> s (m u)").bitcast(F32)
+                woven = h_in[i][:].rearrange("s m u -> s (m u)").bitcast(F32)
                 nc.scalar.copy(out=woven.rearrange("s (m v) -> s m v", v=2), in_=turned[:].rearrange("s v m -> s m v"))
             else:
-                nc.vector.tensor_tensor(out=h_in[j][:, g, :, :], in0=tanh[i][:, g, :, :], in1=ts_wt[j][:, g, :, :], op=MULT)
+                nc.vector.tensor_tensor(out=h_in[i][:], in0=tanh[i][:], in1=ts_wt[i][:], op=MULT)
 
         def quantize_h(i):
-            j, g = divmod(i, G)
-            if g == 0:
-                h_codes[j] = passing("h_codes", [P, G, P], U32)
-                h_scales[j] = passing("h_scales", [P, G, P], U8)
-            nc.vector.quantize_mx(out=h_codes[j][:, g, :].bitcast(E5M2), scales=h_scales[j][:, g, :],
-                                  in_=h_in[j][:, g, :, :].rearrange("s m u -> s (m u)"))
-
-        def quantize_late_kn(g):
-            if g < G:
-                quantize_kn(LAST // 2, g)
+            h_codes[i] = passing("h_codes", [P, P], U32, bufs=len(UNITS))
+            h_scales[i] = passing("h_scales", [P, P], U8, bufs=len(UNITS))
+            nc.vector.quantize_mx(out=h_codes[i][:].bitcast(E5M2), scales=h_scales[i][:],
+                                  in_=h_in[i][:].rearrange("s m u -> s (m u)"))
 
         def empty(j, cols):
             nc.scalar.copy(out=out_f32[j // 2][:, j % 2, cols].rearrange("m (p t) -> m p t", t=PACK),
@@ -266,22 +261,21 @@ def tile_attend_gpq_pl_lch_x_kernel(tc, xT, cb, norm, ts, y, wt, offs, out_0, ou
             nc.sync.dma_start(out=out_rows[:, j, :], in_=out_f32[j // 2][:, j % 2, :])
 
         def back(i):
-            j, g = divmod(i, G)
+            j, g = UNITS[i]
             if g == 0:
                 sums[j] = bank_tile("sums", [P, D], (SUM_BANKS + SCORE_BANKS)[j])
-            nc.tensor.matmul_mx(out=sums[j][:], lhsT=h_codes[j][:, g, :].bitcast(E5M2), lhsT_scale=h_scales[j][:, g, :],
+            nc.tensor.matmul_mx(out=sums[j][:], lhsT=h_codes[i][:].bitcast(E5M2), lhsT_scale=h_scales[i][:],
                                 rhs=kn_codes[:, g, :].bitcast(E4M3), rhs_scale=kn_scales[g][:],
                                 start=(g == 0), stop=(g == G - 1))
             if g == G - 1 and j < LAST:
                 empty(j, slice(0, D))
                 store(j)
 
-        stages = ((score, AHEAD), (subtract, 0), (scale, 1), (squash, 0), (weigh, -WEIGH_BEHIND),
-                  (quantize_h, -QUANTIZE_BEHIND), (quantize_late_kn, -KN_BEHIND), (back, -BACK_BEHIND),
-                  (deal_y, AHEAD + 1), (turn_y, AHEAD))
-        for step in range(-AHEAD - 1, UNITS + BACK_BEHIND):
+        stages = ((weigh, -WEIGH_BEHIND), (scale, SCORE_AHEAD - 1), (quantize_h, -QUANTIZE_BEHIND), (squash, 0),
+                  (deal_y, DEAL_AHEAD), (score, SCORE_AHEAD), (back, -BACK_BEHIND), (turn_y, 1), (subtract, 1))
+        for step in range(-DEAL_AHEAD, len(UNITS) + BACK_BEHIND):
             for stage, distance in stages:
-                if 0 <= step + distance < UNITS:
+                if 0 <= step + distance < len(UNITS):
                     stage(step + distance)
 
         out_in = held("out_in", [P, D, PACK], BF16)

@@ -31,11 +31,12 @@ SCORE_BANKS = (0, 1, 2)
 DIFF_BANKS = (3, 4, 5)
 SUM_BANKS = (6, 7)
 
-SCORE_AHEAD = len(SCORE_BANKS)
-DEAL_AHEAD = SCORE_AHEAD + 1
+TURN_AHEAD = 1
+SCALE_AHEAD = 2
+LEAD = 4
 WEIGH_BEHIND = 3
-QUANTIZE_BEHIND = 5
-BACK_BEHIND = 7
+QUANTIZE_BEHIND = 6
+BACK_BEHIND = len(UNITS) - 1
 
 
 def tile_attend_gpq_pl_lch_x_kernel(tc, xT, cb, norm, ts, y, wt, offs, out_0, out_1, out_2):
@@ -214,14 +215,16 @@ def tile_attend_gpq_pl_lch_x_kernel(tc, xT, cb, norm, ts, y, wt, offs, out_0, ou
                     nc.tensor.matmul(diff[i][:, u, :], lhsT=y_places[i][:, u, :], rhs=ident[:], is_transpose=True,
                                      start=(u == 0), stop=False)
 
+        def turn_scores(i):
+            if i >= ROW_UNITS:
+                for u in range(PACK):
+                    nc.tensor.matmul(diff[i][:, u, :], lhsT=scaled[i][:, u, :], rhs=ident[:], is_transpose=True,
+                                     start=False, stop=(u == PACK - 1))
+
         def subtract(i):
             if i < ROW_UNITS:
                 diff[i] = passing("z_rows", [P, PASS], F32)
                 nc.vector.tensor_tensor(out=diff[i][:], in0=scaled[i][:], in1=y_half(i), op=SUBTRACT)
-            else:
-                for u in range(PACK):
-                    nc.tensor.matmul(diff[i][:, u, :], lhsT=scaled[i][:, u, :], rhs=ident[:], is_transpose=True,
-                                     start=False, stop=(u == PACK - 1))
 
         def squash(i):
             if i < ROW_UNITS:
@@ -232,7 +235,7 @@ def tile_attend_gpq_pl_lch_x_kernel(tc, xT, cb, norm, ts, y, wt, offs, out_0, ou
                 nc.scalar.activation(out=tanh[i][:], in_=diff[i][:].rearrange("s u m -> s m u"), func=ACT.Tanh, scale=-1.0)
 
         def weigh(i):
-            j, g = UNITS[i]
+            j = UNITS[i][0]
             h_in[i] = passing("h_in", [P, P, PACK], BF16, bufs=len(UNITS))
             if i < ROW_UNITS:
                 h_rows = passing("h_rows", [P, PASS], BF16)
@@ -271,9 +274,10 @@ def tile_attend_gpq_pl_lch_x_kernel(tc, xT, cb, norm, ts, y, wt, offs, out_0, ou
                 empty(j, slice(0, D))
                 store(j)
 
-        stages = ((weigh, -WEIGH_BEHIND), (scale, SCORE_AHEAD - 1), (quantize_h, -QUANTIZE_BEHIND), (squash, 0),
-                  (deal_y, DEAL_AHEAD), (score, SCORE_AHEAD), (back, -BACK_BEHIND), (turn_y, 1), (subtract, 1))
-        for step in range(-DEAL_AHEAD, len(UNITS) + BACK_BEHIND):
+        stages = ((back, -BACK_BEHIND), (quantize_h, -QUANTIZE_BEHIND), (weigh, -WEIGH_BEHIND), (subtract, 0),
+                  (squash, 0), (turn_y, TURN_AHEAD), (turn_scores, TURN_AHEAD), (scale, SCALE_AHEAD), (score, LEAD),
+                  (deal_y, LEAD))
+        for step in range(-LEAD, len(UNITS) + BACK_BEHIND):
             for stage, distance in stages:
                 if 0 <= step + distance < len(UNITS):
                     stage(step + distance)
@@ -290,9 +294,9 @@ def tile_attend_gpq_pl_lch_x_kernel(tc, xT, cb, norm, ts, y, wt, offs, out_0, ou
         fourths = [slice(q * D // 4, (q + 1) * D // 4) for q in range(4)]
         for cols in fourths:
             empty(LAST, cols)
-        for cols in fourths[:LAST]:
+        for cols in fourths[:-1]:
             weave_out(LAST // 2, cols)
-        weave_out(LAST // 2, fourths[LAST], nc.scalar.copy)
+        weave_out(LAST // 2, fourths[-1], nc.scalar.copy)
         store(LAST)
 
         words = out_1[0].rearrange("m d j -> m (d j)").bitcast(I32)

@@ -25,6 +25,7 @@ G = N // PASS
 UNITS = ((0, 0), (1, 0), (0, 1), (1, 1)) + tuple((j, g) for j in range(2, PACK) for g in range(G))
 ROW_UNITS = 2
 SUM_UNITS = len(UNITS) - ROW_UNITS
+EARLY_UNIT = ROW_UNITS
 LAST = PACK - 1
 
 SCORE_BANKS = (0, 1, 2)
@@ -142,13 +143,15 @@ def tile_attend_gpq_pl_lch_x_kernel(tc, xT, cb, norm, ts, y, wt, offs, out_0, ou
         kn_codes = held("kn_codes", [P, G, D], U32, on="plane2")
         kn_scales = [held("kn_scales%d" % g, [P, D], U8) for g in range(G)]
 
-        def quantize_kn(pair, g):
-            cols = slice(2 * pair * P, 2 * (pair + 1) * P)
+        def quantize_kn(g, first, count):
+            cols = slice(first * P, (first + count) * P)
+            woven = kn_in[first // 2][g][:, first % 2:first % 2 + count, :, :]
             nc.vector.quantize_mx(out=kn_codes[:, g, cols].bitcast(E4M3), scales=kn_scales[g][:, cols],
-                                  in_=kn_in[pair][g][:].rearrange("s e p u -> s (e p u)"))
+                                  in_=woven.rearrange("s e p u -> s (e p u)"))
 
         for g in range(G):
-            quantize_kn(0, g)
+            quantize_kn(g, 0, 2)
+        quantize_kn(0, 2, 1)
         for g in range(G):
             gather(LAST, g)
 
@@ -176,8 +179,8 @@ def tile_attend_gpq_pl_lch_x_kernel(tc, xT, cb, norm, ts, y, wt, offs, out_0, ou
         quantize_kd(1)
         for g in range(G):
             turn_k(LAST, g)
-        for g in range(G):
-            quantize_kn(LAST // 2, g)
+        quantize_kn(0, LAST, 1)
+        quantize_kn(1, 2, 2)
 
         scores, scaled, y_places, diff, tanh, h_in, h_codes, h_scales, sums = {}, {}, {}, {}, {}, {}, {}, {}, {}
         out_f32 = [held("out_f32_%d" % pair, [P, 2, D], F32) for pair in range(2)]
@@ -204,16 +207,20 @@ def tile_attend_gpq_pl_lch_x_kernel(tc, xT, cb, norm, ts, y, wt, offs, out_0, ou
                                         in1=neg_ts_places[UNITS[i][1]][:], op=MULT)
 
         def deal_y(i):
-            if i >= ROW_UNITS:
-                y_places[i] = passing("y_places", [P, PACK, P], F32, bufs=SUM_UNITS)
+            if i > EARLY_UNIT:
+                y_places[i] = passing("y_places", [P, PACK, P], F32, bufs=SUM_UNITS - 1)
                 nc.scalar.copy(out=y_places[i][:].rearrange("m u s -> m s u"), in_=y_half(i).rearrange("m (s u) -> m s u", u=PACK))
 
         def turn_y(i):
-            if i >= ROW_UNITS:
-                diff[i] = bank_tile("diff", [P, PACK, P], DIFF_BANKS[i % len(DIFF_BANKS)])
-                for u in range(PACK):
-                    nc.tensor.matmul(diff[i][:, u, :], lhsT=y_places[i][:, u, :], rhs=ident[:], is_transpose=True,
-                                     start=(u == 0), stop=False)
+            places = y_half(i).rearrange("m (s u) -> m u s", u=PACK) if i == EARLY_UNIT else y_places[i][:]
+            diff[i] = bank_tile("diff", [P, PACK, P], DIFF_BANKS[i % len(DIFF_BANKS)])
+            for u in range(PACK):
+                nc.tensor.matmul(diff[i][:, u, :], lhsT=places[:, u, :], rhs=ident[:], is_transpose=True,
+                                 start=(u == 0), stop=False)
+
+        def turn_dealt_y(i):
+            if i > EARLY_UNIT:
+                turn_y(i)
 
         def turn_scores(i):
             if i >= ROW_UNITS:
@@ -275,8 +282,9 @@ def tile_attend_gpq_pl_lch_x_kernel(tc, xT, cb, norm, ts, y, wt, offs, out_0, ou
                 store(j)
 
         stages = ((back, -BACK_BEHIND), (quantize_h, -QUANTIZE_BEHIND), (weigh, -WEIGH_BEHIND), (subtract, 0),
-                  (squash, 0), (turn_y, TURN_AHEAD), (turn_scores, TURN_AHEAD), (scale, SCALE_AHEAD), (score, LEAD),
+                  (squash, 0), (turn_dealt_y, TURN_AHEAD), (turn_scores, TURN_AHEAD), (scale, SCALE_AHEAD), (score, LEAD),
                   (deal_y, LEAD))
+        turn_y(EARLY_UNIT)
         for step in range(-LEAD, len(UNITS) + BACK_BEHIND):
             for stage, distance in stages:
                 if 0 <= step + distance < len(UNITS):

@@ -193,7 +193,8 @@ def tile_attend_gpq_pl_lch_x_kernel(tc, xT, cb, norm, ts, y, wt, offs, out_0, ou
         def score(i):
             j, g = UNITS[i]
             cols = slice(j * P, (j + 1) * P)
-            scores[i] = bank_tile("scores", [P, PASS], SCORE_BANKS[i % len(SCORE_BANKS)])
+            banks = SCORE_BANKS + SUM_BANKS[:1]
+            scores[i] = bank_tile("scores", [P, PASS], banks[i % len(banks)])
             nc.tensor.matmul_mx(out=scores[i][:], lhsT=x_codes[:, cols].bitcast(E4M3), lhsT_scale=x_scales[:, cols],
                                 rhs=kd_codes[g][:].bitcast(E4M3), rhs_scale=kd_scales[g][:], start=True, stop=True)
 
@@ -231,7 +232,8 @@ def tile_attend_gpq_pl_lch_x_kernel(tc, xT, cb, norm, ts, y, wt, offs, out_0, ou
         def subtract(i):
             if i < ROW_UNITS:
                 diff[i] = passing("z_rows", [P, PASS], F32)
-                nc.vector.tensor_tensor(out=diff[i][:], in0=scaled[i][:], in1=y_half(i), op=SUBTRACT)
+                engine = nc.gpsimd if i == ROW_UNITS - 1 else nc.vector
+                engine.tensor_tensor(out=diff[i][:], in0=scaled[i][:], in1=y_half(i), op=SUBTRACT)
 
         def squash(i):
             if i < ROW_UNITS:

@@ -36,7 +36,8 @@ TURN_AHEAD = 1
 SCALE_AHEAD = 2
 LEAD = 4
 WEIGH_BEHIND = 3
-QUANTIZE_BEHIND = 6
+QUANTIZE_BEHIND = 5
+QUANTIZE_ROWS_BEHIND = 6
 BACK_BEHIND = len(UNITS) - 1
 
 
@@ -240,7 +241,7 @@ def tile_attend_gpq_pl_lch_x_kernel(tc, xT, cb, norm, ts, y, wt, offs, out_0, ou
                 tanh[i] = passing("tanh_rows", [P, PASS], F32)
                 nc.scalar.activation(out=tanh[i][:], in_=diff[i][:], func=ACT.Tanh)
             else:
-                tanh[i] = passing("tanh_woven", [P, P, PACK], F32, bufs=SUM_UNITS)
+                tanh[i] = held("tanh_woven%d" % i, [P, P, PACK], F32)
                 nc.scalar.activation(out=tanh[i][:], in_=diff[i][:].rearrange("s u m -> s m u"), func=ACT.Tanh, scale=-1.0)
 
         def weigh(i):
@@ -265,6 +266,16 @@ def tile_attend_gpq_pl_lch_x_kernel(tc, xT, cb, norm, ts, y, wt, offs, out_0, ou
             nc.vector.quantize_mx(out=h_codes[i][:].bitcast(E5M2), scales=h_scales[i][:],
                                   in_=h_in[i][:].rearrange("s m u -> s (m u)"))
 
+        def quantize_rows(i):
+            if i < ROW_UNITS:
+                quantize_h(i)
+
+        def quantize_sums(i):
+            if ROW_UNITS <= i < len(UNITS) - 2:
+                quantize_h(i)
+            if i == len(UNITS) - 3:
+                quantize_h(i + 1)
+
         def empty(j, cols):
             nc.scalar.copy(out=out_f32[j // 2][:, j % 2, cols].rearrange("m (p t) -> m p t", t=PACK),
                            in_=sums[j][:].rearrange("m (t p) -> m p t", t=PACK)[:, cols.start // PACK:cols.stop // PACK, :])
@@ -283,16 +294,16 @@ def tile_attend_gpq_pl_lch_x_kernel(tc, xT, cb, norm, ts, y, wt, offs, out_0, ou
                 empty(j, slice(0, D))
                 store(j)
 
-        stages = ((back, -BACK_BEHIND), (quantize_h, -QUANTIZE_BEHIND), (weigh, -WEIGH_BEHIND), (subtract, 0),
+        stages = ((back, -BACK_BEHIND), (quantize_rows, -QUANTIZE_ROWS_BEHIND), (quantize_sums, -QUANTIZE_BEHIND), (weigh, -WEIGH_BEHIND), (subtract, 0),
                   (squash, 0), (turn_dealt_y, TURN_AHEAD), (turn_scores, TURN_AHEAD), (scale, SCALE_AHEAD), (score, LEAD),
                   (deal_y, LEAD))
         turn_y(EARLY_UNIT)
-        for step in range(-LEAD, len(UNITS) + BACK_BEHIND):
+        for step in range(-LEAD, len(UNITS) + BACK_BEHIND - 1):
             for stage, distance in stages:
                 if 0 <= step + distance < len(UNITS):
                     stage(step + distance)
 
-        out_in = held("out_in", [P, D, PACK], BF16)
+        out_in = held("out_in", [P, D, PACK], BF16, on="tanh_woven%d" % (len(UNITS) - 2))
         out_codes = held("out_codes", [P, D], U32)
         out_scales = held("out_scales", [P, D], U8)
         halves = [slice(half * D // 2, (half + 1) * D // 2) for half in range(2)]
@@ -300,7 +311,10 @@ def tile_attend_gpq_pl_lch_x_kernel(tc, xT, cb, norm, ts, y, wt, offs, out_0, ou
         def weave_out(pair, cols, copy=nc.vector.tensor_copy):
             copy(out=out_in[:, cols, 2 * pair:2 * pair + 2], in_=out_f32[pair][:, :, cols].rearrange("m e d -> m d e"))
 
-        weave_out(0, slice(0, D))
+        weave_out(0, halves[0])
+        quantize_h(len(UNITS) - 1)
+        back(len(UNITS) - 1)
+        weave_out(0, halves[1])
         fourths = [slice(q * D // 4, (q + 1) * D // 4) for q in range(4)]
         for cols in fourths:
             empty(LAST, cols)

@@ -113,7 +113,7 @@ def tile_attend_gpq_pl_lch_x_kernel(tc, xT, cb, norm, ts, y, wt, offs, out_0, ou
 
         k_f32 = [[held("k_f32_%d_%d" % (pair, g), [P, 2, PASS], F32) for g in range(G)] for pair in range(2)]
         kd_in = [held("kd_in%d" % g, [P, PASS, PACK], BF16) for g in range(G)]
-        kn_in = [[held("kn_in_%d_%d" % (pair, g), [P, 2, P, PACK], BF16) for g in range(G)] for pair in range(2)]
+        kn_in = [[held("kn_in_%d_%d" % (pair, g), [P, 2, 2, P // 2, PACK], BF16) for g in range(G)] for pair in range(2)]
 
         def gather(t, g):
             list_cols = PASS // 16
@@ -130,7 +130,7 @@ def tile_attend_gpq_pl_lch_x_kernel(tc, xT, cb, norm, ts, y, wt, offs, out_0, ou
             places = k_f32[t // 2][g][:, t % 2, :].rearrange("p (s u) -> p u s", u=PACK)
             for u in range(PACK):
                 nc.tensor.transpose(turned[:, u, :], places[:, u, :], ident[:])
-            nc.scalar.copy(out=kn_in[t // 2][g][:, t % 2, :, :], in_=turned[:].rearrange("s u p -> s p u"))
+            nc.scalar.copy(out=kn_in[t // 2][g][:, :, t % 2, :, :], in_=turned[:].rearrange("s u (h p) -> s h p u", h=2))
 
         for t in range(LAST):
             for g in range(G):
@@ -145,10 +145,11 @@ def tile_attend_gpq_pl_lch_x_kernel(tc, xT, cb, norm, ts, y, wt, offs, out_0, ou
         kn_scales = [held("kn_scales%d" % g, [P, D], U8) for g in range(G)]
 
         def quantize_kn(g, first, count):
-            cols = slice(first * P, (first + count) * P)
-            woven = kn_in[first // 2][g][:, first % 2:first % 2 + count, :, :]
-            nc.vector.quantize_mx(out=kn_codes[:, g, cols].bitcast(E4M3), scales=kn_scales[g][:, cols],
-                                  in_=woven.rearrange("s e p u -> s (e p u)"))
+            for half in range(2):
+                cols = slice(half * D // 2 + first * P // 2, half * D // 2 + (first + count) * P // 2)
+                woven = kn_in[first // 2][g][:, half, first % 2:first % 2 + count, :, :]
+                nc.vector.quantize_mx(out=kn_codes[:, g, cols].bitcast(E4M3), scales=kn_scales[g][:, cols],
+                                      in_=woven.rearrange("s e p u -> s (e p u)"))
 
         for g in range(G):
             quantize_kn(g, 0, 2)
@@ -271,53 +272,57 @@ def tile_attend_gpq_pl_lch_x_kernel(tc, xT, cb, norm, ts, y, wt, offs, out_0, ou
                 quantize_h(i)
 
         def quantize_sums(i):
-            if ROW_UNITS <= i < len(UNITS) - 2:
+            if i >= ROW_UNITS:
                 quantize_h(i)
-            if i == len(UNITS) - 3:
-                quantize_h(i + 1)
 
-        def empty(j, cols):
-            nc.scalar.copy(out=out_f32[j // 2][:, j % 2, cols].rearrange("m (p t) -> m p t", t=PACK),
-                           in_=sums[j][:].rearrange("m (t p) -> m p t", t=PACK)[:, cols.start // PACK:cols.stop // PACK, :])
+        halves = [slice(half * D // 2, (half + 1) * D // 2) for half in range(2)]
+
+        def empty(j):
+            nc.scalar.copy(out=out_f32[j // 2][:, j % 2, :].rearrange("m (h p t) -> m h p t", h=2, t=PACK),
+                           in_=sums[j][:].rearrange("m (h t p) -> m h p t", h=2, t=PACK))
+
+        def empty_fourth(q):
+            rows = slice(q % 2 * P // 4, (q % 2 + 1) * P // 4)
+            nc.scalar.copy(out=out_f32[LAST // 2][:, LAST % 2, q * D // 4:(q + 1) * D // 4].rearrange("m (p t) -> m p t", t=PACK),
+                           in_=sums[LAST, q // 2][:].rearrange("m (t p) -> m p t", t=PACK)[:, rows, :])
 
         def store(j):
             nc.sync.dma_start(out=out_rows[:, j, :], in_=out_f32[j // 2][:, j % 2, :])
 
         def back(i):
             j, g = UNITS[i]
-            if g == 0:
-                sums[j] = bank_tile("sums", [P, D], (SUM_BANKS + SCORE_BANKS)[j])
-            nc.tensor.matmul_mx(out=sums[j][:], lhsT=h_codes[i][:].bitcast(E5M2), lhsT_scale=h_scales[i][:],
-                                rhs=kn_codes[:, g, :].bitcast(E4M3), rhs_scale=kn_scales[g][:],
-                                start=(g == 0), stop=(g == G - 1))
+            banks = SUM_BANKS + SCORE_BANKS
+            parts = [(j, slice(0, D), banks[j])] if j < LAST else [((j, half), halves[half], banks[j + half]) for half in range(2)]
+            for key, cols, bank in parts:
+                if g == 0:
+                    sums[key] = bank_tile("sums", [P, cols.stop - cols.start], bank)
+                nc.tensor.matmul_mx(out=sums[key][:], lhsT=h_codes[i][:].bitcast(E5M2), lhsT_scale=h_scales[i][:],
+                                    rhs=kn_codes[:, g, cols].bitcast(E4M3), rhs_scale=kn_scales[g][:, cols],
+                                    start=(g == 0), stop=(g == G - 1))
             if g == G - 1 and j < LAST:
-                empty(j, slice(0, D))
+                empty(j)
                 store(j)
 
         stages = ((back, -BACK_BEHIND), (quantize_rows, -QUANTIZE_ROWS_BEHIND), (quantize_sums, -QUANTIZE_BEHIND), (weigh, -WEIGH_BEHIND), (subtract, 0),
                   (squash, 0), (turn_dealt_y, TURN_AHEAD), (turn_scores, TURN_AHEAD), (scale, SCALE_AHEAD), (score, LEAD),
                   (deal_y, LEAD))
         turn_y(EARLY_UNIT)
-        for step in range(-LEAD, len(UNITS) + BACK_BEHIND - 1):
+        for step in range(-LEAD, len(UNITS) + BACK_BEHIND):
             for stage, distance in stages:
                 if 0 <= step + distance < len(UNITS):
                     stage(step + distance)
 
-        out_in = held("out_in", [P, D, PACK], BF16, on="tanh_woven%d" % (len(UNITS) - 2))
+        out_in = held("out_in", [P, D, PACK], BF16, on="tanh_woven%d" % (len(UNITS) - 1))
         out_codes = held("out_codes", [P, D], U32)
         out_scales = held("out_scales", [P, D], U8)
-        halves = [slice(half * D // 2, (half + 1) * D // 2) for half in range(2)]
 
         def weave_out(pair, cols, copy=nc.vector.tensor_copy):
             copy(out=out_in[:, cols, 2 * pair:2 * pair + 2], in_=out_f32[pair][:, :, cols].rearrange("m e d -> m d e"))
 
-        weave_out(0, halves[0])
-        quantize_h(len(UNITS) - 1)
-        back(len(UNITS) - 1)
-        weave_out(0, halves[1])
+        weave_out(0, slice(0, D))
         fourths = [slice(q * D // 4, (q + 1) * D // 4) for q in range(4)]
-        for cols in fourths:
-            empty(LAST, cols)
+        for q in range(4):
+            empty_fourth(q)
         for cols in fourths[:-1]:
             weave_out(LAST // 2, cols)
         weave_out(LAST // 2, fourths[-1], nc.scalar.copy)

@@ -49,7 +49,7 @@ def tile_attend_gpq_pl_lch_x_kernel(tc, xT, cb, norm, ts, y, wt, offs, out_0, ou
         psum = ctx.enter_context(tc.psum_pool(name="psum", bufs=1))
 
         def held(name, shape, dtype, on=""):
-            return keep.tile(shape, dtype, name=name, tag=on or name, align_bytes=64)
+            return keep.tile(shape, dtype, name=name, tag=on or name, align_bytes=256)
 
         def passing(name, shape, dtype, bufs=None):
             return ring.tile(shape, dtype, name=name, align_bytes=64, bufs=bufs)

@@ -58,8 +58,8 @@ def tile_attend_gpq_pl_lch_x_kernel(tc, xT, cb, norm, ts, y, wt, offs, out_0, ou
             return psum.tile(shape, F32, name=name, tag="bank%d" % bank)
 
         wt_col = held("wt_col", [P, PACK], F32)
-        ts_col = held("ts_col", [P, G, PACK], F32)
-        norm_col = held("norm_col", [P, G, PACK], F32)
+        ts_col = held("ts_col", [P, G, 2 * PACK], F32)[:, :, 0:PACK]
+        norm_col = held("norm_col", [P, G, 2 * PACK], F32)[:, :, 0:PACK]
         offsets = keep.tile([P, N // 16], U16, name="offsets")
         planes = [held("plane%d" % t, [P, C], F32) for t in range(PACK)]
         x_raw = [held("x_raw%d" % half, [P, PACK, R // 2], F32) for half in range(2)]
@@ -69,9 +69,9 @@ def tile_attend_gpq_pl_lch_x_kernel(tc, xT, cb, norm, ts, y, wt, offs, out_0, ou
         y_rows = y.rearrange("(m j) n -> m j n", j=PACK)
 
         nc.sync.dma_start(out=wt_col[:], in_=wt.rearrange("(m j) o -> m (j o)", j=PACK))
-        nc.sync.dma_start(out=ts_col[:], in_=ts[0, :].rearrange("(g s u) -> s g u", g=G, u=PACK))
-        nc.sync.dma_start(out=norm_col[:], in_=norm[0, :].rearrange("(g s u) -> s g u", g=G, u=PACK))
+        nc.sync.dma_start(out=ts_col, in_=ts[0, :].rearrange("(g s u) -> s g u", g=G, u=PACK))
         nc.sync.dma_start(out=planes[0][:], in_=cb_rows[:, 0, :])
+        nc.sync.dma_start(out=norm_col, in_=norm[0, :].rearrange("(g s u) -> s g u", g=G, u=PACK))
         nc.sync.dma_start(offsets[:], offs)
         for t in range(1, PACK):
             nc.sync.dma_start(out=planes[t][:], in_=cb_rows[:, t, :])
@@ -95,10 +95,10 @@ def tile_attend_gpq_pl_lch_x_kernel(tc, xT, cb, norm, ts, y, wt, offs, out_0, ou
         norm_row = [held("norm_row%d" % g, [P, PASS], F32) for g in range(G)]
         ts_row = held("ts_row", [P, PASS], F32)
         neg_ts_places = [held("neg_ts_places%d" % g, [P, PACK, P], F32) for g in range(G)]
+        wt_rows = spread(wt_col, DIFF_BANKS[0])
         for g in range(G):
             rows = spread(norm_col[:, g, :], SCORE_BANKS[g])
             nc.scalar.copy(out=in_column_order(norm_row[g]), in_=rows[:].rearrange("q u s -> q s u"))
-        wt_rows = spread(wt_col, DIFF_BANKS[0])
         ts_wt = {}
         for i in range(ROW_UNITS, len(UNITS)):
             j, g = UNITS[i]

@@ -26,6 +26,7 @@ UNITS = ((0, 0), (1, 0), (0, 1), (1, 1)) + tuple((j, g) for j in range(2, PACK) 
 ROW_UNITS = 2
 SUM_UNITS = len(UNITS) - ROW_UNITS
 EARLY_UNIT = ROW_UNITS
+RUN = N // P
 LAST = PACK - 1
 
 SCORE_BANKS = (0, 1, 2)
@@ -58,8 +59,8 @@ def tile_attend_gpq_pl_lch_x_kernel(tc, xT, cb, norm, ts, y, wt, offs, out_0, ou
             return psum.tile(shape, F32, name=name, tag="bank%d" % bank)
 
         wt_col = held("wt_col", [P, PACK], F32)
-        ts_col = held("ts_col", [P, G, 2 * PACK], F32)[:, :, 0:PACK]
-        norm_col = held("norm_col", [P, G, 2 * PACK], F32)[:, :, 0:PACK]
+        ts_runs = held("ts_runs", [P, RUN], F32)
+        norm_runs = held("norm_runs", [P, RUN], F32)
         offsets = keep.tile([P, N // 16], U16, name="offsets")
         planes = [held("plane%d" % t, [P, C], F32) for t in range(PACK)]
         x_raw = [held("x_raw%d" % half, [P, PACK, R // 2], F32) for half in range(2)]
@@ -68,10 +69,10 @@ def tile_attend_gpq_pl_lch_x_kernel(tc, xT, cb, norm, ts, y, wt, offs, out_0, ou
         x_rows = xT.rearrange("(p t) r -> p t r", t=PACK)
         y_rows = y.rearrange("(m j) n -> m j n", j=PACK)
 
+        nc.sync.dma_start(out=ts_runs[:], in_=ts[0, :].rearrange("(q c) -> q c", c=RUN))
         nc.sync.dma_start(out=wt_col[:], in_=wt.rearrange("(m j) o -> m (j o)", j=PACK))
-        nc.sync.dma_start(out=ts_col, in_=ts[0, :].rearrange("(g s u) -> s g u", g=G, u=PACK))
+        nc.sync.dma_start(out=norm_runs[:], in_=norm[0, :].rearrange("(q c) -> q c", c=RUN))
         nc.sync.dma_start(out=planes[0][:], in_=cb_rows[:, 0, :])
-        nc.sync.dma_start(out=norm_col, in_=norm[0, :].rearrange("(g s u) -> s g u", g=G, u=PACK))
         nc.sync.dma_start(offsets[:], offs)
         for t in range(1, PACK):
             nc.sync.dma_start(out=planes[t][:], in_=cb_rows[:, t, :])
@@ -89,29 +90,39 @@ def tile_attend_gpq_pl_lch_x_kernel(tc, xT, cb, norm, ts, y, wt, offs, out_0, ou
                 nc.tensor.transpose(rows[:, u, :], columns[:, u:u + 1].to_broadcast([P, P]), ident[:])
             return rows
 
-        def in_column_order(tile):
-            return tile[:].rearrange("q (s u) -> q s u", u=PACK)
+        def as_row(name, runs, banks, copies):
+            row = held(name, [P, N], F32)
+            for part, (bank, copy) in enumerate(zip(banks, copies)):
+                cols = slice(part * PACK, (part + 1) * PACK)
+                copy(out=row[:].rearrange("a (q c) -> a q c", c=RUN)[:, :, cols],
+                     in_=spread(runs[:, cols], bank)[:].rearrange("a c q -> a q c"))
+            return [row[:, g * PASS:(g + 1) * PASS] for g in range(G)]
 
-        norm_row = [held("norm_row%d" % g, [P, PASS], F32) for g in range(G)]
-        ts_row = held("ts_row", [P, PASS], F32)
-        neg_ts_places = [held("neg_ts_places%d" % g, [P, PACK, P], F32) for g in range(G)]
-        wt_rows = spread(wt_col, DIFF_BANKS[0])
-        for g in range(G):
-            rows = spread(norm_col[:, g, :], SCORE_BANKS[g])
-            nc.scalar.copy(out=in_column_order(norm_row[g]), in_=rows[:].rearrange("q u s -> q s u"))
-        ts_wt = {}
-        for i in range(ROW_UNITS, len(UNITS)):
-            j, g = UNITS[i]
-            ts_wt[i] = held("ts_wt%d" % i, [P, P, PACK], F32)
-            nc.vector.tensor_tensor(out=ts_wt[i][:], in0=wt_rows[:, j, :].unsqueeze(2).to_broadcast([P, P, PACK]),
-                                    in1=ts_col[:, g, :].unsqueeze(1).to_broadcast([P, P, PACK]), op=MULT)
-        for g in range(G):
-            rows = spread(ts_col[:, g, :], SUM_BANKS[g])
-            nc.scalar.activation(out=neg_ts_places[g][:], in_=rows[:], func=ACT.Copy, scale=-1.0)
-            if g == 0:
-                nc.scalar.copy(out=in_column_order(ts_row), in_=rows[:].rearrange("q u s -> q s u"))
-
+        ts_rows = as_row("ts_rows", ts_runs, SUM_BANKS, (nc.scalar.copy, nc.vector.tensor_copy))
+        ts_row = ts_rows[0]
         k_f32 = [[held("k_f32_%d_%d" % (pair, g), [P, 2, PASS], F32) for g in range(G)] for pair in range(2)]
+        wt_rows = k_f32[0][0][:, 1, :].rearrange("a (j m) -> a j m", j=PACK)
+        nc.scalar.copy(out=wt_rows, in_=spread(wt_col, DIFF_BANKS[0])[:])
+        ts_places = [row.rearrange("a (s u) -> a u s", u=PACK) for row in ts_rows]
+        ts_wt = {}
+
+        def tables(g):
+            ts_turned = bank_tile("ts_turned", [P, PACK, P], SCORE_BANKS[g])
+            for u in range(PACK):
+                nc.tensor.transpose(ts_turned[:, u, :], ts_places[g][:, u, :], ident[:])
+            for i in range(ROW_UNITS, len(UNITS)):
+                if UNITS[i][1] == g:
+                    ts_wt[i] = held("ts_wt%d" % i, [P, P, PACK], F32)
+                    nc.vector.tensor_tensor(out=ts_wt[i][:], in0=ts_turned[:].rearrange("s u m -> s m u"),
+                                            in1=wt_rows[:, UNITS[i][0], :].unsqueeze(2).to_broadcast([P, P, PACK]), op=MULT)
+
+        tables(1)
+        norm_row = as_row("norm_rows", norm_runs, SUM_BANKS, (nc.scalar.copy, nc.scalar.copy))
+        tables(0)
+        neg_ts_places = [held("neg_ts_places%d" % g, [P, PACK, P], F32) for g in range(G)]
+        for g in range(G):
+            nc.scalar.activation(out=neg_ts_places[g][:], in_=ts_places[g], func=ACT.Copy, scale=-1.0)
+
         kd_in = [held("kd_in%d" % g, [P, PASS, PACK], BF16) for g in range(G)]
         kn_in = [[held("kn_in_%d_%d" % (pair, g), [P, 2, 2, P // 2, PACK], BF16) for g in range(G)] for pair in range(2)]
 
@@ -120,7 +131,7 @@ def tile_attend_gpq_pl_lch_x_kernel(tc, xT, cb, norm, ts, y, wt, offs, out_0, ou
             nc.vector.tensor_tensor(
                 out=k_f32[t // 2][g][:, t % 2, :],
                 in0=planes[t][:].indirect(offsets[:, g * list_cols:(g + 1) * list_cols]),
-                in1=norm_row[g][:], op=MULT)
+                in1=norm_row[g], op=MULT)
 
         def weave_k(pair, g, copy):
             copy(out=kd_in[g][:, :, 2 * pair:2 * pair + 2], in_=k_f32[pair][g][:].rearrange("p e n -> p n e"))
@@ -185,7 +196,7 @@ def tile_attend_gpq_pl_lch_x_kernel(tc, xT, cb, norm, ts, y, wt, offs, out_0, ou
         quantize_kn(1, 2, 2)
 
         scores, scaled, y_places, diff, tanh, h_in, h_codes, h_scales, sums = {}, {}, {}, {}, {}, {}, {}, {}, {}
-        out_f32 = [held("out_f32_%d" % pair, [P, 2, D], F32) for pair in range(2)]
+        out_f32 = [held("out_f32_%d" % pair, [P, 2, D], F32, on="plane%d" % pair) for pair in range(2)]
         out_rows = out_0.rearrange("(m j) d -> m j d", j=PACK)
 
         def y_half(i):
@@ -203,7 +214,7 @@ def tile_attend_gpq_pl_lch_x_kernel(tc, xT, cb, norm, ts, y, wt, offs, out_0, ou
         def scale(i):
             if i < ROW_UNITS:
                 scaled[i] = passing("a_rows", [P, PASS], F32)
-                nc.vector.tensor_tensor(out=scaled[i][:], in0=scores[i][:], in1=ts_row[:], op=MULT)
+                nc.vector.tensor_tensor(out=scaled[i][:], in0=scores[i][:], in1=ts_row, op=MULT)
             else:
                 scaled[i] = passing("neg_a", [P, PACK, P], F32, bufs=SUM_UNITS)
                 nc.vector.tensor_tensor(out=scaled[i][:], in0=scores[i][:].rearrange("m (s u) -> m u s", u=PACK),
@@ -250,7 +261,7 @@ def tile_attend_gpq_pl_lch_x_kernel(tc, xT, cb, norm, ts, y, wt, offs, out_0, ou
             h_in[i] = passing("h_in", [P, P, PACK], BF16, bufs=len(UNITS))
             if i < ROW_UNITS:
                 h_rows = passing("h_rows", [P, PASS], BF16)
-                nc.vector.scalar_tensor_tensor(out=h_rows[:], in0=tanh[i][:], scalar=wt_col[:, j:j + 1], in1=ts_row[:],
+                nc.vector.scalar_tensor_tensor(out=h_rows[:], in0=tanh[i][:], scalar=wt_col[:, j:j + 1], in1=ts_row,
                                                op0=MULT, op1=MULT)
                 pairs = h_rows[:].bitcast(F32).rearrange("m (s v) -> m v s", v=2)
                 turned = bank_tile("turned_h", [P, 2, P], SUM_BANKS[1])

@@ -36,10 +36,10 @@ SUM_BANKS = (6, 7)
 TURN_AHEAD = 1
 SCALE_AHEAD = 2
 LEAD = 4
-WEIGH_BEHIND = 3
-QUANTIZE_BEHIND = 5
-QUANTIZE_ROWS_BEHIND = 6
-BACK_BEHIND = len(UNITS) - 1
+WEIGH_BEHIND = 4
+QUANTIZE_BEHIND = 6
+QUANTIZE_ROWS_BEHIND = 7
+BACK_BEHIND = len(UNITS)
 
 
 def tile_attend_gpq_pl_lch_x_kernel(tc, xT, cb, norm, ts, y, wt, offs, out_0, out_1, out_2):

from contextlib import ExitStack

import concourse.mybir as mybir
from concourse.masks import make_identity

N, C, D, R = 1024, 4096, 512, 512
FLOPS = 2 * 2 * R * N * D

F32 = mybir.dt.float32
BF16 = mybir.dt.bfloat16
U32 = mybir.dt.uint32
I32 = mybir.dt.int32
U16 = mybir.dt.uint16
U8 = mybir.dt.uint8
E4M3 = mybir.dt.float8_e4m3fn_x4
E5M2 = mybir.dt.float8_e5m2_x4
MULT = mybir.AluOpType.mult
SUBTRACT = mybir.AluOpType.subtract
ACT = mybir.ActivationFunctionType

P = 128
PACK = 4
PASS = P * PACK
G = N // PASS
UNITS = ((0, 0), (1, 0), (0, 1), (1, 1)) + tuple((j, g) for j in range(2, PACK) for g in range(G))
ROW_UNITS = 2
SUM_UNITS = len(UNITS) - ROW_UNITS
EARLY_UNIT = ROW_UNITS
RUN = N // P
LAST = PACK - 1

SCORE_BANKS = (0, 1, 2)
DIFF_BANKS = (3, 4, 5)
SUM_BANKS = (6, 7)

TURN_AHEAD = 1
SCALE_AHEAD = 2
LEAD = 4
WEIGH_BEHIND = 4
QUANTIZE_BEHIND = 6
QUANTIZE_ROWS_BEHIND = 7
BACK_BEHIND = len(UNITS)


def tile_attend_gpq_pl_lch_x_kernel(tc, xT, cb, norm, ts, y, wt, offs, out_0, out_1, out_2):
    nc = tc.nc
    with ExitStack() as ctx:
        keep = ctx.enter_context(tc.tile_pool(name="keep", bufs=1))
        ring = ctx.enter_context(tc.tile_pool(name="ring", bufs=ROW_UNITS))
        psum = ctx.enter_context(tc.psum_pool(name="psum", bufs=1))

        def held(name, shape, dtype, on=""):
            return keep.tile(shape, dtype, name=name, tag=on or name, align_bytes=256)

        def passing(name, shape, dtype, bufs=None):
            return ring.tile(shape, dtype, name=name, align_bytes=64, bufs=bufs)

        def bank_tile(name, shape, bank):
            return psum.tile(shape, F32, name=name, tag="bank%d" % bank)

        wt_col = held("wt_col", [P, PACK], F32)
        ts_runs = held("ts_runs", [P, RUN], F32)
        norm_runs = held("norm_runs", [P, RUN], F32)
        offsets = keep.tile([P, N // 16], U16, name="offsets")
        planes = [held("plane%d" % t, [P, C], F32) for t in range(PACK)]
        x_raw = [held("x_raw%d" % half, [P, PACK, R // 2], F32) for half in range(2)]
        y_raw = [held("y_raw%d" % j, [P, N], F32) for j in range(PACK)]
        cb_rows = cb.rearrange("(p t) c -> p t c", t=PACK)
        x_rows = xT.rearrange("(p t) r -> p t r", t=PACK)
        y_rows = y.rearrange("(m j) n -> m j n", j=PACK)

        nc.sync.dma_start(out=ts_runs[:], in_=ts[0, :].rearrange("(q c) -> q c", c=RUN))
        nc.sync.dma_start(out=wt_col[:], in_=wt.rearrange("(m j) o -> m (j o)", j=PACK))
        nc.sync.dma_start(out=norm_runs[:], in_=norm[0, :].rearrange("(q c) -> q c", c=RUN))
        nc.sync.dma_start(out=planes[0][:], in_=cb_rows[:, 0, :])
        nc.sync.dma_start(offsets[:], offs)
        for t in range(1, PACK):
            nc.sync.dma_start(out=planes[t][:], in_=cb_rows[:, t, :])
        for half in range(2):
            nc.sync.dma_start(out=x_raw[half][:], in_=x_rows[:, :, half * R // 2:(half + 1) * R // 2])
        for j in range(PACK):
            nc.sync.dma_start(out=y_raw[j][:], in_=y_rows[:, j, :])

        ident = held("ident", [P, P], F32)
        make_identity(nc, ident[:])

        def spread(columns, bank):
            rows = bank_tile("rows", [P, PACK, P], bank)
            for u in range(PACK):
                nc.tensor.transpose(rows[:, u, :], columns[:, u:u + 1].to_broadcast([P, P]), ident[:])
            return rows

        def as_row(name, runs, banks, copies):
            row = held(name, [P, N], F32)
            for part, (bank, copy) in enumerate(zip(banks, copies)):
                cols = slice(part * PACK, (part + 1) * PACK)
                copy(out=row[:].rearrange("a (q c) -> a q c", c=RUN)[:, :, cols],
                     in_=spread(runs[:, cols], bank)[:].rearrange("a c q -> a q c"))
            return [row[:, g * PASS:(g + 1) * PASS] for g in range(G)]

        ts_rows = as_row("ts_rows", ts_runs, SUM_BANKS, (nc.scalar.copy, nc.vector.tensor_copy))
        ts_row = ts_rows[0]
        k_f32 = [[held("k_f32_%d_%d" % (pair, g), [P, 2, PASS], F32) for g in range(G)] for pair in range(2)]
        wt_rows = k_f32[0][0][:, 1, :].rearrange("a (j m) -> a j m", j=PACK)
        nc.scalar.copy(out=wt_rows, in_=spread(wt_col, DIFF_BANKS[0])[:])
        ts_places = [row.rearrange("a (s u) -> a u s", u=PACK) for row in ts_rows]
        ts_wt = {}

        def tables(g):
            ts_turned = bank_tile("ts_turned", [P, PACK, P], SCORE_BANKS[g])
            for u in range(PACK):
                nc.tensor.transpose(ts_turned[:, u, :], ts_places[g][:, u, :], ident[:])
            for i in range(ROW_UNITS, len(UNITS)):
                if UNITS[i][1] == g:
                    ts_wt[i] = held("ts_wt%d" % i, [P, P, PACK], F32)
                    nc.vector.tensor_tensor(out=ts_wt[i][:], in0=ts_turned[:].rearrange("s u m -> s m u"),
                                            in1=wt_rows[:, UNITS[i][0], :].unsqueeze(2).to_broadcast([P, P, PACK]), op=MULT)

        tables(1)
        norm_row = as_row("norm_rows", norm_runs, SUM_BANKS, (nc.scalar.copy, nc.scalar.copy))
        tables(0)
        neg_ts_places = [held("neg_ts_places%d" % g, [P, PACK, P], F32) for g in range(G)]
        for g in range(G):
            nc.scalar.activation(out=neg_ts_places[g][:], in_=ts_places[g], func=ACT.Copy, scale=-1.0)

        kd_in = [held("kd_in%d" % g, [P, PASS, PACK], BF16) for g in range(G)]
        kn_in = [[held("kn_in_%d_%d" % (pair, g), [P, 2, 2, P // 2, PACK], BF16) for g in range(G)] for pair in range(2)]

        def gather(t, g):
            list_cols = PASS // 16
            nc.vector.tensor_tensor(
                out=k_f32[t // 2][g][:, t % 2, :],
                in0=planes[t][:].indirect(offsets[:, g * list_cols:(g + 1) * list_cols]),
                in1=norm_row[g], op=MULT)

        def weave_k(pair, g, copy):
            copy(out=kd_in[g][:, :, 2 * pair:2 * pair + 2], in_=k_f32[pair][g][:].rearrange("p e n -> p n e"))

        def turn_k(t, g):
            turned = bank_tile("turned_k", [P, PACK, P], (DIFF_BANKS[1:], SUM_BANKS)[t % 2][g])
            places = k_f32[t // 2][g][:, t % 2, :].rearrange("p (s u) -> p u s", u=PACK)
            for u in range(PACK):
                nc.tensor.transpose(turned[:, u, :], places[:, u, :], ident[:])
            nc.scalar.copy(out=kn_in[t // 2][g][:, :, t % 2, :, :], in_=turned[:].rearrange("s u (h p) -> s h p u", h=2))

        for t in range(LAST):
            for g in range(G):
                gather(t, g)
            for g in range(G):
                turn_k(t, g)
            if t % 2 == 1:
                for g in range(G):
                    weave_k(t // 2, g, nc.scalar.copy)

        kn_codes = held("kn_codes", [P, G, D], U32, on="plane2")
        kn_scales = [held("kn_scales%d" % g, [P, D], U8) for g in range(G)]

        def quantize_kn(g, first, count):
            for half in range(2):
                cols = slice(half * D // 2 + first * P // 2, half * D // 2 + (first + count) * P // 2)
                woven = kn_in[first // 2][g][:, half, first % 2:first % 2 + count, :, :]
                nc.vector.quantize_mx(out=kn_codes[:, g, cols].bitcast(E4M3), scales=kn_scales[g][:, cols],
                                      in_=woven.rearrange("s e p u -> s (e p u)"))

        for g in range(G):
            quantize_kn(g, 0, 2)
        quantize_kn(0, 2, 1)
        for g in range(G):
            gather(LAST, g)

        x_in = held("x_in", [P, PACK, P, PACK], BF16)
        x_codes = held("x_codes", [P, R], U32)
        x_scales = held("x_scales", [P, R], U8)
        for half, copy in enumerate((nc.scalar.copy, nc.vector.tensor_copy)):
            copy(out=x_in[:, :, half * P // 2:(half + 1) * P // 2, :].rearrange("p j m t -> p m t j"),
                 in_=x_raw[half][:].rearrange("p t (m j) -> p m t j", j=PACK))
        for g, copy in enumerate((nc.vector.tensor_copy, nc.scalar.copy)):
            weave_k(LAST // 2, g, copy)

        kd_codes = [held("kd_codes0", [P, PASS], U32, on="x_raw0"), held("kd_codes1", [P, PASS], U32)]
        kd_scales = [held("kd_scales%d" % g, [P, PASS], U8) for g in range(G)]

        def quantize_kd(g):
            nc.vector.quantize_mx(out=kd_codes[g][:].bitcast(E4M3), scales=kd_scales[g][:],
                                  in_=kd_in[g][:].rearrange("p n t -> p (n t)"))

        quantize_kd(0)
        for pair in range(2):
            cols = slice(2 * pair * P, 2 * (pair + 1) * P)
            nc.vector.quantize_mx(out=x_codes[:, cols].bitcast(E4M3), scales=x_scales[:, cols],
                                  in_=x_in[:, 2 * pair:2 * pair + 2, :, :].rearrange("p j m t -> p (j m t)"))
        quantize_kd(1)
        for g in range(G):
            turn_k(LAST, g)
        quantize_kn(0, LAST, 1)
        quantize_kn(1, 2, 2)

        scores, scaled, y_places, diff, tanh, h_in, h_codes, h_scales, sums = {}, {}, {}, {}, {}, {}, {}, {}, {}
        out_f32 = [held("out_f32_%d" % pair, [P, 2, D], F32, on="plane%d" % pair) for pair in range(2)]
        out_rows = out_0.rearrange("(m j) d -> m j d", j=PACK)

        def y_half(i):
            j, g = UNITS[i]
            return y_raw[j][:, g * PASS:(g + 1) * PASS]

        def score(i):
            j, g = UNITS[i]
            cols = slice(j * P, (j + 1) * P)
            banks = SCORE_BANKS + SUM_BANKS[:1]
            scores[i] = bank_tile("scores", [P, PASS], banks[i % len(banks)])
            nc.tensor.matmul_mx(out=scores[i][:], lhsT=x_codes[:, cols].bitcast(E4M3), lhsT_scale=x_scales[:, cols],
                                rhs=kd_codes[g][:].bitcast(E4M3), rhs_scale=kd_scales[g][:], start=True, stop=True)

        def scale(i):
            if i < ROW_UNITS:
                scaled[i] = passing("a_rows", [P, PASS], F32)
                nc.vector.tensor_tensor(out=scaled[i][:], in0=scores[i][:], in1=ts_row, op=MULT)
            else:
                scaled[i] = passing("neg_a", [P, PACK, P], F32, bufs=SUM_UNITS)
                nc.vector.tensor_tensor(out=scaled[i][:], in0=scores[i][:].rearrange("m (s u) -> m u s", u=PACK),
                                        in1=neg_ts_places[UNITS[i][1]][:], op=MULT)

        def deal_y(i):
            if i > EARLY_UNIT:
                y_places[i] = passing("y_places", [P, PACK, P], F32, bufs=SUM_UNITS - 1)
                nc.scalar.copy(out=y_places[i][:].rearrange("m u s -> m s u"), in_=y_half(i).rearrange("m (s u) -> m s u", u=PACK))

        def turn_y(i):
            places = y_half(i).rearrange("m (s u) -> m u s", u=PACK) if i == EARLY_UNIT else y_places[i][:]
            diff[i] = bank_tile("diff", [P, PACK, P], DIFF_BANKS[i % len(DIFF_BANKS)])
            for u in range(PACK):
                nc.tensor.matmul(diff[i][:, u, :], lhsT=places[:, u, :], rhs=ident[:], is_transpose=True,
                                 start=(u == 0), stop=False)

        def turn_dealt_y(i):
            if i > EARLY_UNIT:
                turn_y(i)

        def turn_scores(i):
            if i >= ROW_UNITS:
                for u in range(PACK):
                    nc.tensor.matmul(diff[i][:, u, :], lhsT=scaled[i][:, u, :], rhs=ident[:], is_transpose=True,
                                     start=False, stop=(u == PACK - 1))

        def subtract(i):
            if i < ROW_UNITS:
                diff[i] = passing("z_rows", [P, PASS], F32)
                engine = nc.gpsimd if i == ROW_UNITS - 1 else nc.vector
                engine.tensor_tensor(out=diff[i][:], in0=scaled[i][:], in1=y_half(i), op=SUBTRACT)

        def squash(i):
            if i < ROW_UNITS:
                tanh[i] = passing("tanh_rows", [P, PASS], F32)
                nc.scalar.activation(out=tanh[i][:], in_=diff[i][:], func=ACT.Tanh)
            else:
                tanh[i] = held("tanh_woven%d" % i, [P, P, PACK], F32)
                nc.scalar.activation(out=tanh[i][:], in_=diff[i][:].rearrange("s u m -> s m u"), func=ACT.Tanh, scale=-1.0)

        def weigh(i):
            j = UNITS[i][0]
            h_in[i] = passing("h_in", [P, P, PACK], BF16, bufs=len(UNITS))
            if i < ROW_UNITS:
                h_rows = passing("h_rows", [P, PASS], BF16)
                nc.vector.scalar_tensor_tensor(out=h_rows[:], in0=tanh[i][:], scalar=wt_col[:, j:j + 1], in1=ts_row,
                                               op0=MULT, op1=MULT)
                pairs = h_rows[:].bitcast(F32).rearrange("m (s v) -> m v s", v=2)
                turned = bank_tile("turned_h", [P, 2, P], SUM_BANKS[1])
                for v in range(2):
                    nc.tensor.transpose(turned[:, v, :], pairs[:, v, :], ident[:])
                woven = h_in[i][:].rearrange("s m u -> s (m u)").bitcast(F32)
                nc.scalar.copy(out=woven.rearrange("s (m v) -> s m v", v=2), in_=turned[:].rearrange("s v m -> s m v"))
            else:
                nc.vector.tensor_tensor(out=h_in[i][:], in0=tanh[i][:], in1=ts_wt[i][:], op=MULT)

        def quantize_h(i):
            h_codes[i] = passing("h_codes", [P, P], U32, bufs=len(UNITS))
            h_scales[i] = passing("h_scales", [P, P], U8, bufs=len(UNITS))
            nc.vector.quantize_mx(out=h_codes[i][:].bitcast(E5M2), scales=h_scales[i][:],
                                  in_=h_in[i][:].rearrange("s m u -> s (m u)"))

        def quantize_rows(i):
            if i < ROW_UNITS:
                quantize_h(i)

        def quantize_sums(i):
            if i >= ROW_UNITS:
                quantize_h(i)

        halves = [slice(half * D // 2, (half + 1) * D // 2) for half in range(2)]

        def empty(j):
            nc.scalar.copy(out=out_f32[j // 2][:, j % 2, :].rearrange("m (h p t) -> m h p t", h=2, t=PACK),
                           in_=sums[j][:].rearrange("m (h t p) -> m h p t", h=2, t=PACK))

        def empty_fourth(q):
            rows = slice(q % 2 * P // 4, (q % 2 + 1) * P // 4)
            nc.scalar.copy(out=out_f32[LAST // 2][:, LAST % 2, q * D // 4:(q + 1) * D // 4].rearrange("m (p t) -> m p t", t=PACK),
                           in_=sums[LAST, q // 2][:].rearrange("m (t p) -> m p t", t=PACK)[:, rows, :])

        def store(j):
            nc.sync.dma_start(out=out_rows[:, j, :], in_=out_f32[j // 2][:, j % 2, :])

        def back(i):
            j, g = UNITS[i]
            banks = SUM_BANKS + SCORE_BANKS
            parts = [(j, slice(0, D), banks[j])] if j < LAST else [((j, half), halves[half], banks[j + half]) for half in range(2)]
            for key, cols, bank in parts:
                if g == 0:
                    sums[key] = bank_tile("sums", [P, cols.stop - cols.start], bank)
                nc.tensor.matmul_mx(out=sums[key][:], lhsT=h_codes[i][:].bitcast(E5M2), lhsT_scale=h_scales[i][:],
                                    rhs=kn_codes[:, g, cols].bitcast(E4M3), rhs_scale=kn_scales[g][:, cols],
                                    start=(g == 0), stop=(g == G - 1))
            if g == G - 1 and j < LAST:
                empty(j)
                store(j)

        stages = ((back, -BACK_BEHIND), (quantize_rows, -QUANTIZE_ROWS_BEHIND), (quantize_sums, -QUANTIZE_BEHIND), (weigh, -WEIGH_BEHIND), (subtract, 0),
                  (squash, 0), (turn_dealt_y, TURN_AHEAD), (turn_scores, TURN_AHEAD), (scale, SCALE_AHEAD), (score, LEAD),
                  (deal_y, LEAD))
        turn_y(EARLY_UNIT)
        for step in range(-LEAD, len(UNITS) + BACK_BEHIND):
            for stage, distance in stages:
                if 0 <= step + distance < len(UNITS):
                    stage(step + distance)

        out_in = held("out_in", [P, D, PACK], BF16, on="tanh_woven%d" % (len(UNITS) - 1))
        out_codes = held("out_codes", [P, D], U32)
        out_scales = held("out_scales", [P, D], U8)

        def weave_out(pair, cols, copy=nc.vector.tensor_copy):
            copy(out=out_in[:, cols, 2 * pair:2 * pair + 2], in_=out_f32[pair][:, :, cols].rearrange("m e d -> m d e"))

        weave_out(0, slice(0, D))
        fourths = [slice(q * D // 4, (q + 1) * D // 4) for q in range(4)]
        for q in range(4):
            empty_fourth(q)
        for cols in fourths[:-1]:
            weave_out(LAST // 2, cols)
        weave_out(LAST // 2, fourths[-1], nc.scalar.copy)
        store(LAST)

        words = out_1[0].rearrange("m d j -> m (d j)").bitcast(I32)
        for cols in halves:
            nc.vector.quantize_mx(out=out_codes[:, cols].bitcast(E4M3), scales=out_scales[:, cols],
                                  in_=out_in[:, cols, :].rearrange("m d j -> m (d j)"))
            nc.scalar.dma_start(out=words[:, cols], in_=out_codes[:, cols].bitcast(I32))
        for q in range(4):
            queue = nc.scalar if q % 2 else nc.sync
            queue.dma_start(out=out_2[0, 4 * q:4 * q + 4, :].bitcast(I32), in_=out_scales[32 * q:32 * q + 4, :].bitcast(I32))
